import numpy as np
import ml_dtypes


def mxq(x, axis, fmt="e4m3"):
    dtype, down = {"e4m3": (ml_dtypes.float8_e4m3fn, 7), "e5m2": (ml_dtypes.float8_e5m2, 14)}[fmt]
    v = np.moveaxis(np.asarray(x, np.float32).astype(ml_dtypes.bfloat16).astype(np.float64), axis, -1)
    blocks = v.reshape(v.shape[:-1] + (-1, 32))
    amax = np.abs(blocks).max(-1, keepdims=True)
    byte = np.maximum(np.where(amax > 0, np.frexp(amax)[1] - 1 + 127, 0) - down, 1)
    scale = np.exp2(byte - 127.0)
    codes = (blocks / scale).astype(np.float32).astype(dtype).astype(np.float64)
    return np.moveaxis((codes * scale).reshape(v.shape), -1, axis)


WIDE = False


def mx_kscale(k):
    if not WIDE:
        return np.ones(k)
    levels = np.array([24, -24, 12, -12, 0])
    if k % 512:
        return np.exp2(np.random.permutation(np.resize(levels, k // 32))).repeat(32)
    a = np.empty((k // 512, 16))
    for p in range(k // 512):
        a[p, :8] = np.random.permutation(np.resize(levels, 8))
        for g in range(8):
            far = levels[np.abs(levels - a[p, g]) >= 10]
            a[p, g + 8] = far[np.random.randint(len(far))]
    return np.exp2(a.ravel()).repeat(32)


def f64(x):
    return np.asarray(x).astype(np.float64)


def striped(idx):
    return np.tile(idx.reshape(-1, 16).T, (8, 1)).astype(np.uint16)


def unstriped(offs):
    return offs[:16].T.reshape(-1).astype(np.int64)


E2M1 = np.array([0.0, 0.5, 1.0, 1.5, 2.0, 3.0, 4.0, 6.0, -0.0, -0.5, -1.0, -1.5, -2.0, -3.0, -4.0, -6.0])


def pack_weight(w, fmt):
    k, n = w.shape
    w = f64(np.asarray(w, np.float32).astype(ml_dtypes.bfloat16)).reshape(k // 32, 32, n)
    amax = np.abs(w).max(1)
    if fmt == "e4m3":
        byte = np.frexp(amax)[1] - 1 + 127 - 7
    else:
        mant, ex = np.frexp(amax / 6.0)
        byte = np.where(mant > 0.5, ex, ex - 1) + 127
    byte = np.clip(np.where(amax > 0, byte, 1), 1, 254)
    scaled = (w * np.exp2(127.0 - byte)[:, None, :]).reshape(k, n).astype(np.float32)
    by_word = np.ascontiguousarray(scaled.reshape(k // 512, 128, 4, n).transpose(0, 1, 3, 2))
    if fmt == "e4m3":
        words = by_word.astype(ml_dtypes.float8_e4m3fn).view(np.uint8)
    else:
        c = by_word.astype(ml_dtypes.float4_e2m1fn).view(np.uint8) & 0xF
        words = (c[..., 0::2] | (c[..., 1::2] << 4)).reshape(k // 512, 128, 2 * n)
    return np.ascontiguousarray(words), np.ascontiguousarray(byte.astype(np.uint8).reshape(k // 512, 16, n))


def unpack_weight(words, scales, fmt):
    g, _, n = scales.shape
    words = np.ascontiguousarray(words).reshape(g, 128, n, -1)
    if fmt == "e4m3":
        vals = words.view(ml_dtypes.float8_e4m3fn).astype(np.float64)
    else:
        nib = np.empty((g, 128, n, 4), np.uint8)
        nib[..., 0::2] = words & 0xF
        nib[..., 1::2] = words >> 4
        vals = E2M1[nib]
    vals = vals * np.repeat(np.exp2(scales.astype(np.float64) - 127.0), 8, axis=1)[..., None]
    return vals.transpose(0, 1, 3, 2).reshape(g * 512, n)


def pack_table4(v):
    words, scales = pack_weight(v, "e2m1")
    g, t = words.shape[0] // 2, v.shape[1]
    return np.ascontiguousarray(words.reshape(g, 2, 128, t, 2).transpose(0, 2, 3, 1, 4).reshape(g, 128, t, 4)), scales


def unpack_table4(words, scales):
    g, _, t, _ = words.shape
    return unpack_weight(words.reshape(g, 128, t, 2, 2).transpose(0, 3, 1, 2, 4).reshape(2 * g, 128, 2 * t), scales, "e2m1")


def planes(y):
    n, m = y.shape
    v = y.astype(np.float32).astype(ml_dtypes.bfloat16).astype(np.float64).reshape(n // 32, 32, m)
    top = np.abs(v).max(1)
    byte = np.clip(np.where(top > 0, np.frexp(top)[1] - 1 + 127 - 7, 1), 1, 254)
    codes = (v * np.exp2(127.0 - byte)[:, None, :]).reshape(n, m).astype(np.float32).astype(ml_dtypes.float8_e4m3fn).view(np.uint8)
    words = codes.reshape(n // 512, 128, 4, m).transpose(0, 1, 3, 2)
    return np.ascontiguousarray(words), np.ascontiguousarray(byte.astype(np.uint8).reshape(n // 512, 16, m))


def sigm(f):
    return 1.0 / (1.0 + np.exp(-np.maximum(f, -700.0)))


K, M, N, T, J = 512, 1024, 1024, 2048, 1024


def setup_inputs():
    n = np.random.standard_normal
    s = mx_kscale(K)[:, None]
    s2 = mx_kscale(M)[:, None]
    h = np.tanh(n((N, T)))
    p_tab = pack_table4(h * s2)
    p_wz = pack_weight(n((K, N)) / np.sqrt(K) / s, "e4m3")
    p_wr = pack_weight(n((K, N)) / np.sqrt(K) / s, "e4m3")
    p_wn = pack_weight(n((K, N)) / np.sqrt(K) / s, "e4m3")
    return {
        "x": (n((K, J)) * s).astype(np.float32),
        "tab_words": p_tab[0],
        "tab_scales": p_tab[1],
        "wz_words": p_wz[0],
        "wz_scales": p_wz[1],
        "uz": (n((M, N)) / np.sqrt(M) / s2).astype(np.float32),
        "wr_words": p_wr[0],
        "wr_scales": p_wr[1],
        "ur": (n((M, N)) / np.sqrt(M) / s2).astype(np.float32),
        "wn_words": p_wn[0],
        "wn_scales": p_wn[1],
        "un": (n((M, N)) / np.sqrt(M) / s2).astype(np.float32),
        "bz": (0.3 * n(N)).astype(np.float32),
        "br": (0.3 * n(N)).astype(np.float32),
        "bn": (0.3 * n(N)).astype(np.float32),
        "hT": (h).astype(np.float32),
        "wgo": np.tile(np.random.uniform(0.5, 2.0, J), (128, 1)).astype(np.float32),
        "offs": striped(np.random.permutation(T)[:J]),
    }


def reference(x, tab_words, tab_scales, wz_words, wz_scales, uz, wr_words, wr_scales, ur, wn_words, wn_scales, un, bz, br, bn, hT, wgo, offs):
    idx = unstriped(offs)
    x_ = mxq(f64(x), 0, "e4m3")
    tab_ = unpack_table4(tab_words, tab_scales)[:, idx]
    wz_ = unpack_weight(wz_words, wz_scales, "e4m3")
    uz_ = mxq(f64(uz), 0, "e4m3")
    wr_ = unpack_weight(wr_words, wr_scales, "e4m3")
    ur_ = mxq(f64(ur), 0, "e4m3")
    wn_ = unpack_weight(wn_words, wn_scales, "e4m3")
    un_ = mxq(f64(un), 0, "e4m3")
    sz = wz_.T @ x_ + uz_.T @ tab_
    z = sigm(sz + f64(bz)[:, None])
    sr = wr_.T @ x_ + ur_.T @ tab_
    r = sigm(sr + f64(br)[:, None])
    xn = wn_.T @ x_
    hn = un_.T @ tab_
    cd = np.tanh(xn + f64(bn)[:, None] + r * hn)
    out = np.zeros((N, T))
    out[:, idx] = f64(wgo)[0] * (f64(hT)[:, idx] + z * (cd - f64(hT)[:, idx]))
    return (out,) + planes(out)

@@ -1,0 +1,434 @@
+from contextlib import ExitStack
+
+import concourse.mybir as mybir
+from concourse.masks import make_identity
+
+K, M, N, T, J = 512, 1024, 1024, 2048, 1024
+FLOPS = 2 * 3 * (K + M) * N * J
+
+F32 = mybir.dt.float32
+BF16 = mybir.dt.bfloat16
+I32 = mybir.dt.int32
+U32 = mybir.dt.uint32
+U16 = mybir.dt.uint16
+U8 = mybir.dt.uint8
+FP8X4 = mybir.dt.float8_e4m3fn_x4
+FP4X4 = mybir.dt.float4_e2m1fn_x4
+ACT = mybir.ActivationFunctionType
+ALU = mybir.AluOpType
+
+P = 128
+PACK = 4
+HALF = 512
+HALVES = J // HALF
+TILES = N // P
+STEPS = TILES * HALVES
+PASSES = M // 512
+QUADS = 4
+CHUNKS = [(0, 128), (128, 128), (256, 256), (512, 256), (768, 256)]
+WINDOWS = 3
+R, C, Z = 0, 1, 2
+
+
+def tile_list_tgn_gruP_kernel(
+    tc, x, tab_words, tab_scales, wz_words, wz_scales, uz, wr_words, wr_scales, ur,
+    wn_words, wn_scales, un, bz, br, bn, hT, wgo, offs, out_0, out_1, out_2,
+):
+    nc = tc.nc
+    w_words_dram = [wr_words, wn_words, wz_words]
+    w_scales_dram = [wr_scales, wn_scales, wz_scales]
+    u_dram = [ur, un, uz]
+    b_dram = [br, bn, bz]
+
+    with ExitStack() as ctx:
+        keep = ctx.enter_context(tc.tile_pool(name="keep", bufs=1))
+        ring = ctx.enter_context(tc.tile_pool(name="ring", bufs=2))
+        psum = ctx.enter_context(tc.psum_pool(name="psum", bufs=1))
+
+        offsets = keep.tile([P, J // 16], U16, name="offsets")
+        nc.sync.dma_start(offsets[:], offs)
+
+        def offs_of(h):
+            return offsets[:, h * (HALF // 16) : (h + 1) * (HALF // 16)]
+
+        table_scales = keep.tile([P, PASSES, T], U8, name="table_scales", align_bytes=64)
+        nc.vector.memset(table_scales[:].rearrange("p a t -> p (a t)").bitcast(I32), 0)
+        w_scales = [keep.tile([P, N], U8, name="w_scales%d" % g, align_bytes=64) for g in (R, C, Z)]
+        for g in (R, C, Z):
+            nc.vector.memset(w_scales[g][:].bitcast(I32), 0)
+        bias_rows = keep.tile([P, P], F32, name="bias_rows")
+        nc.vector.memset(bias_rows[:], 0.0)
+        warm = keep.tile([P, 16], F32, name="warm")
+        nc.vector.memset(warm[:, 0:8], 0.0)
+        nc.scalar.activation(out=warm[:, 8:16], in_=warm[:, 0:8], func=ACT.Sigmoid)
+
+        table_words = keep.tile([P, T], U32, name="table_words")
+        nc.sync.dma_start(table_words[:].bitcast(I32), tab_words[0].rearrange("p t b -> p (t b)").bitcast(I32))
+        for q in range(QUADS):
+            nc.gpsimd.dma_start(
+                table_scales[32 * q : 32 * q + 4, :, :].bitcast(I32),
+                tab_scales[:, 4 * q : 4 * q + 4, :].rearrange("a r t -> r a t").bitcast(I32),
+            )
+        ident = keep.tile([P, P], F32, name="ident")
+        make_identity(nc, ident[:])
+
+        def load_w_scales(queue, g, q):
+            queue.dma_start(
+                w_scales[g][32 * q : 32 * q + 4, :].bitcast(I32),
+                w_scales_dram[g][0, 4 * q : 4 * q + 4, :].bitcast(I32),
+            )
+
+        for g in (R, Z):
+            for q in range(QUADS):
+                load_w_scales(nc.gpsimd, g, q)
+        windows = [keep.tile([P, T], F32, name="window%d" % w) for w in range(WINDOWS)]
+        nc.vector.memset(windows[0][:], 0.0)
+        nc.vector.memset(windows[1][:], 0.0)
+        nc.vector.memset(windows[2][:], 0.0)
+
+        x_raw = {}
+
+        def load_x(h):
+            x_raw[h] = keep.tile([P, PACK, HALF], F32, name="x_raw%d" % h)
+            nc.sync.dma_start(x_raw[h][:], x[:, h * HALF : (h + 1) * HALF].rearrange("(p t) j -> p t j", t=PACK))
+
+        u_slots = [[keep.tile([P, PACK * 256], F32, name="u_raw%d_%d" % (k, piece)) for piece in range(6)] for k in range(2)]
+
+        def u_raw(c, piece):
+            n0, width = CHUNKS[c]
+            e0 = PACK * (n0 % 256)
+            return u_slots[(n0 // 256) % 2][piece][:, e0 : e0 + PACK * width].rearrange("p (t n) -> p t n", t=PACK)
+
+        def load_u(c, piece):
+            n0, width = CHUNKS[c]
+            g, a = divmod(piece, PASSES)
+            nc.sync.dma_start(
+                u_raw(c, piece),
+                u_dram[g][512 * a : 512 * (a + 1), n0 : n0 + width].rearrange("(p t) n -> p t n", t=PACK),
+            )
+
+        w_words = {}
+        W_PARTS = [(0, 256), (256, 256), (512, 512)]
+
+        def load_w(g, part):
+            c0, width = W_PARTS[part]
+            w_words[g, part] = keep.tile([P, width], U32, name="w_words%d_%d" % (g, part), align_bytes=64)
+            flat = w_words_dram[g][0].rearrange("p n b -> p (n b)")
+            nc.sync.dma_start(w_words[g, part][:].bitcast(I32), flat[:, 4 * c0 : 4 * (c0 + width)].bitcast(I32))
+
+        state = [keep.tile([P, T], F32, name="state%d" % k) for k in range(3)]
+
+        def load_state(i):
+            nc.sync.dma_start(state[i % 3][:], hT[P * i : P * (i + 1), :])
+
+        def load_bias(g):
+            nc.sync.dma_start(bias_rows[TILES * g : TILES * (g + 1), :], b_dram[g].rearrange("(i p) -> i p", p=P))
+
+        weight = [keep.tile([P, HALF], F32, name="weight%d" % h) for h in range(HALVES)]
+
+        def load_weight(h):
+            nc.sync.dma_start(weight[h][:], wgo[:, h * HALF : (h + 1) * HALF])
+
+        load_x(0)
+        load_u(0, 0)
+        load_u(0, 1)
+        load_w(R, 0)
+        load_u(0, 2)
+        load_u(0, 3)
+        load_bias(R)
+        load_w(C, 0)
+        load_bias(C)
+        load_state(0)
+        load_bias(Z)
+        load_u(0, 4)
+        load_w_scales(nc.sync, C, 0)
+        load_u(0, 5)
+        load_w_scales(nc.sync, C, 1)
+        load_w_scales(nc.sync, C, 2)
+        load_x(1)
+        load_w_scales(nc.sync, C, 3)
+        load_w(Z, 0)
+        load_weight(0)
+        for piece in range(4):
+            load_u(1, piece)
+        load_state(1)
+        load_weight(1)
+        load_u(1, 4)
+        load_u(1, 5)
+        for g in (R, C, Z):
+            load_u(2, 2 * g)
+            load_u(2, 2 * g + 1)
+            load_w(g, 1)
+            if g == C:
+                load_state(2)
+
+        v_codes, v_scales, x_codes, x_scales = {}, {}, {}, {}
+
+        def gather_table(h):
+            picked = keep.tile([P, HALF], U32, name="picked%d" % h)
+            nc.vector.tensor_copy(picked[:], table_words[:].indirect(offs_of(h)))
+            v_codes[h] = keep.tile([P, PASSES, 2 * HALF], U8, name="v_codes%d" % h, align_bytes=64)
+            nc.vector.tensor_copy(
+                v_codes[h][:].bitcast(U16),
+                picked[:].bitcast(U16).rearrange("p (j d) -> p d j", d=PASSES),
+            )
+            for a in range(PASSES):
+                v_scales[h, a] = keep.tile([P, HALF], U8, name="v_scales%d_%d" % (h, a), align_bytes=64)
+                nc.vector.tensor_copy(v_scales[h, a][:], table_scales[:, a, :].indirect(offs_of(h)))
+
+        def interleave(copy, dst, raw):
+            copy(
+                dst.rearrange("p (c i) t -> p c t i", i=4),
+                raw.rearrange("p t (c i) -> p c t i", i=4),
+            )
+
+        def quantize_x(h):
+            x_bf = ring.tile([P, HALF, PACK], BF16, name="x_bf", tag="x_bf", bufs=1, align_bytes=64)
+            interleave(nc.scalar.copy, x_bf[:], x_raw[h][:])
+            x_codes[h] = keep.tile([P, HALF], U32, name="x_codes%d" % h, align_bytes=64)
+            x_scales[h] = keep.tile([P, HALF], U8, name="x_scales%d" % h, align_bytes=64)
+            nc.vector.quantize_mx(
+                out=x_codes[h][:].bitcast(FP8X4), scales=x_scales[h][:],
+                in_=x_bf[:].rearrange("p j t -> p (j t)"),
+            )
+
+        UW = PASSES * P
+        u_bf = [keep.tile([P, 3 * UW * PACK], BF16, name="u_bf%d" % k, align_bytes=64) for k in range(2)]
+        u_codes = [keep.tile([P, 3 * UW], U32, name="u_codes%d" % k, align_bytes=64) for k in range(2)]
+        u_scales = [keep.tile([P, 3 * UW], U8, name="u_scales%d" % k, align_bytes=64) for k in range(2)]
+
+        def chunk_of(i):
+            for c, (n0, width) in enumerate(CHUNKS):
+                if n0 <= P * i < n0 + width:
+                    return c, P * i - n0
+
+        def round_u(i, piece):
+            g, a = divmod(piece, PASSES)
+            c, off = chunk_of(i)
+            c0 = (g * UW + a * P) * PACK
+            dst = u_bf[i % 2][:, c0 : c0 + P * PACK].rearrange("p (n t) -> p n t", t=PACK)
+            interleave(nc.scalar.copy, dst, u_raw(c, piece)[:, :, off : off + P])
+            if i in (1, 3):
+                load_u(c + 2, piece)
+                if i == 1 and a == 1:
+                    load_w(g, 2)
+            if a == PASSES - 1:
+                if i == 0 or g == Z:
+                    quantize_u(i, g, g + 1)
+                elif g == C:
+                    quantize_u(i, R, Z)
+
+        def quantize_u(i, g0, g1):
+            nc.vector.quantize_mx(
+                out=u_codes[i % 2][:, g0 * UW : g1 * UW].bitcast(FP8X4),
+                scales=u_scales[i % 2][:, g0 * UW : g1 * UW],
+                in_=u_bf[i % 2][:, g0 * UW * PACK : g1 * UW * PACK],
+            )
+
+        bias = keep.tile([P, 3 * TILES], F32, name="bias")
+
+        def turn_biases():
+            bank = psum.tile([P, 4, P], F32, name="turned", tag="turned", bufs=2)
+            nc.tensor.transpose(bank[:, 0, :], bias_rows[:], ident[:])
+            nc.scalar.copy(bias[:], bank[:, 0, 0 : 3 * TILES])
+
+        def x_pass(bank, g, i, h, stop):
+            part = min(i // 2, 2)
+            c0 = P * i - W_PARTS[part][0]
+            nc.tensor.matmul_mx(
+                out=bank[:],
+                lhsT=w_words[g, part][:, c0 : c0 + P].bitcast(FP8X4),
+                lhsT_scale=w_scales[g][:, P * i : P * (i + 1)],
+                rhs=x_codes[h][:].bitcast(FP8X4),
+                rhs_scale=x_scales[h][:],
+                start=True, stop=stop,
+            )
+
+        def v_passes(bank, g, i, h, start):
+            for a in range(PASSES):
+                cols = slice(g * UW + a * P, g * UW + (a + 1) * P)
+                nc.tensor.matmul_mx(
+                    out=bank[:],
+                    lhsT=u_codes[i % 2][:, cols].bitcast(FP8X4),
+                    lhsT_scale=u_scales[i % 2][:, cols],
+                    rhs=v_codes[h][:, a, :].bitcast(FP4X4),
+                    rhs_scale=v_scales[h, a][:],
+                    start=(start and a == 0), stop=(a == PASSES - 1),
+                )
+
+        DEPTH = 5
+        Z_DEPTH = 4
+        work = [keep.tile([P, 2 * HALF], F32, name="work%d" % k) for k in range(DEPTH)]
+        z_tiles = [keep.tile([P, HALF], F32, name="z%d" % k) for k in range(Z_DEPTH)]
+
+        def r_of(s):
+            return work[s % DEPTH][:, HALF // 2 : HALF // 2 + HALF]
+
+        def old_of(s):
+            return work[s % DEPTH][:, 0:HALF]
+
+        def new_of(s):
+            if s == 0:
+                return z_of(3)
+            return value_of(s + 3)
+
+        def value_of(s):
+            return work[(s - 1) % DEPTH][:, HALF : 2 * HALF]
+
+        def z_of(s):
+            return z_tiles[s % Z_DEPTH][:]
+
+        def gate(g, s, dst):
+            i, h = divmod(s, HALVES)
+            bank = psum.tile([P, HALF], F32, name="gate_sum", tag="gate_sum%d" % g)
+            x_pass(bank, g, i, h, False)
+            v_passes(bank, g, i, h, False)
+            nc.scalar.activation(
+                out=dst, in_=bank[:], func=ACT.Sigmoid, bias=bias[:, TILES * g + i : TILES * g + i + 1]
+            )
+
+        def front(s):
+            i, h = divmod(s, HALVES)
+            y = value_of(s)
+            hn = psum.tile([P, HALF], F32, name="hn", tag="hn")
+            v_passes(hn, C, i, h, True)
+            xn = psum.tile([P, HALF], F32, name="xn", tag="xn")
+            x_pass(xn, C, i, h, True)
+            nc.vector.tensor_tensor(y, hn[:], r_of(s), ALU.mult)
+            nc.vector.tensor_copy(old_of(s), state[i % 3][:].indirect(offs_of(h)))
+            nc.vector.tensor_tensor(y, xn[:], y, ALU.add)
+
+        def candidate(s):
+            i = s // HALVES
+            nc.scalar.activation(
+                out=value_of(s), in_=value_of(s), func=ACT.Tanh, bias=bias[:, TILES * C + i : TILES * C + i + 1]
+            )
+
+        def blend(s):
+            y = value_of(s)
+            old = old_of(s)
+            nc.gpsimd.tensor_tensor(y, y, old, ALU.subtract)
+            nc.gpsimd.tensor_tensor(y, y, z_of(s), ALU.mult)
+            nc.gpsimd.tensor_tensor(y, y, old, ALU.add)
+
+        def weigh(s):
+            nc.gpsimd.tensor_tensor(new_of(s), value_of(s), weight[s % HALVES][:], ALU.mult)
+
+        def scatter(s):
+            i, h = divmod(s, HALVES)
+            window = windows[i % WINDOWS]
+            nc.vector.tensor_copy(window[:].indirect(offs_of(h)), new_of(s))
+            if h == HALVES - 1:
+                nc.sync.dma_start(out_0[P * i : P * (i + 1), :], window[:])
+
+        y_scales = keep.tile([P, TILES, T // QUADS], U8, name="y_scales", align_bytes=64)
+
+        grouped, backs = {}, {}
+
+        def turn(i, half, tags, copies, place=None):
+            window = windows[i % WINDOWS]
+            backs[i, half] = psum.tile([P, 2, 2, P], F32, name="back", tag="back", bufs=2)
+            for k in range(2):
+                grp = 2 * half + k
+                turned = psum.tile([P, QUADS, P], F32, name="turned", tag=tags[k], bufs=(2 if tags[k] == "turned" else 1))
+                for q in range(QUADS):
+                    t0 = (T // QUADS) * q + P * grp
+                    nc.tensor.transpose(turned[:, q, :], window[:, t0 : t0 + P], ident[:])
+                if place is None:
+                    pairs_tile = ring.tile([P, 2 * P], F32, name="pairs", tag="pairs", bufs=4)
+                    pairs = pairs_tile[:]
+                else:
+                    pairs = place[:, 2 * P * k : 2 * P * (k + 1)]
+                copies[k](
+                    pairs.bitcast(BF16).rearrange("p (u m e) -> p u m e", u=2, e=2),
+                    turned[:].rearrange("p q (m u e) -> p u (q m) e", u=2, e=2),
+                )
+                for u in range(2):
+                    nc.tensor.transpose(backs[i, half][:, k, u, :], pairs[:, P * u : P * (u + 1)], ident[:])
+
+        def group(i, half, copy):
+            if half == 0:
+                grouped[i] = ring.tile([P, 2 * HALF], F32, name="grouped", tag="grouped", bufs=2, align_bytes=64)
+            dst = grouped[i][:, HALF * half : HALF * (half + 1)].rearrange("p (k t u) -> p k t u", k=2, u=2)
+            copy(dst, backs[i, half][:].rearrange("p k u t -> p k t u"))
+
+        words_dram = out_1.rearrange("a p t b -> (a p) (t b)").bitcast(I32)
+
+        def planes(i):
+            y_codes = ring.tile([P, T // QUADS], U32, name="y_codes", tag="y_codes", bufs=3, align_bytes=64)
+            nc.vector.quantize_mx(
+                out=y_codes[:].bitcast(FP8X4), scales=y_scales[:, i, :],
+                in_=grouped[i][:].bitcast(BF16),
+            )
+            for q in range(QUADS):
+                nc.sync.dma_start(
+                    words_dram[32 * i : 32 * (i + 1), (T // QUADS) * q : (T // QUADS) * (q + 1)],
+                    y_codes[32 * q : 32 * (q + 1), :].bitcast(I32),
+                )
+
+        gather_table(0)
+        quantize_x(0)
+        turn_biases()
+        scalar_only = [nc.scalar.copy, nc.scalar.copy]
+        for piece in range(4):
+            round_u(0, piece)
+        gate(R, 0, r_of(0))
+        front(0)
+        candidate(0)
+        round_u(0, 4)
+        round_u(0, 5)
+        gate(Z, 0, z_of(0))
+        blend(0)
+        weigh(0)
+        gather_table(1)
+        quantize_x(1)
+        gate(R, 1, r_of(1))
+        front(1)
+        gate(Z, 1, z_of(1))
+
+        def round_piece(k, j):
+            i, piece = divmod(3 * (k + 7) + j, 3 * PASSES)
+            if i < TILES:
+                round_u(i, piece)
+
+        for k in range(-5, STEPS + 1):
+            if 0 <= k < STEPS:
+                scatter(k)
+            if 2 <= k + 3 < STEPS:
+                front(k + 3)
+            if 1 <= k + 1 < STEPS - 1:
+                weigh(k + 1)
+            if k % 2 == 0 and k >= -2 and k // 2 + 4 < TILES:
+                load_state(k // 2 + 4)
+            if 0 <= k - 3 < STEPS - 2:
+                group((k - 3) // 2, (k - 3) % 2, nc.scalar.copy)
+                if (k - 3) % 2 == 1:
+                    planes((k - 3) // 2)
+            round_piece(k, 0)
+            if 1 <= k + 2 < STEPS:
+                candidate(k + 2)
+                blend(k + 2)
+            if 2 <= k + 3 < STEPS:
+                gate(Z, k + 3, z_of(k + 3))
+            if 2 <= k + 4 < STEPS:
+                gate(R, k + 4, r_of(k + 4))
+            if 0 <= k - 2 < STEPS - 4:
+                turn((k - 2) // 2, (k - 2) % 2, ("turned", "turned"), scalar_only)
+            if k == STEPS - 3:
+                turn(TILES - 2, 0, ("turned", "turned"), scalar_only)
+                turn(TILES - 2, 1, ("turned", "turned"), scalar_only, new_of(STEPS - 1))
+                weigh(STEPS - 1)
+            round_piece(k, 1)
+            round_piece(k, 2)
+        both = [nc.scalar.copy, nc.vector.tensor_copy]
+        turn(TILES - 1, 0, ("turned", "turned"), both)
+        turn(TILES - 1, 1, ("hn", "xn"), both)
+        group(TILES - 1, 0, nc.scalar.copy)
+        group(TILES - 1, 1, nc.vector.tensor_copy)
+        planes(TILES - 1)
+        scales_dram = out_2.rearrange("a (i r) t -> r (a i) t", r=4)
+        for q in range(QUADS):
+            nc.scalar.dma_start(
+                scales_dram[:, :, (T // QUADS) * q : (T // QUADS) * (q + 1)].bitcast(I32),
+                y_scales[32 * q : 32 * q + 4, :, :].bitcast(I32),
+            )

@@ -26,7 +26,7 @@ STEPS = TILES * HALVES
 PASSES = M // 512
 QUADS = 4
 CHUNKS = [(0, 128), (128, 128), (256, 256), (512, 256), (768, 256)]
-WINDOWS = 3
+WINDOWS = 2
 R, C, Z = 0, 1, 2
 
 
@@ -62,7 +62,7 @@ def tile_list_tgn_gruP_kernel(
         nc.vector.memset(warm[:, 0:8], 0.0)
         nc.scalar.activation(out=warm[:, 8:16], in_=warm[:, 0:8], func=ACT.Sigmoid)
 
-        table_words = keep.tile([P, T], U32, name="table_words")
+        table_words = keep.tile([P, T], U32, name="table_words", tag="second_window")
         nc.sync.dma_start(table_words[:].bitcast(I32), tab_words[0].rearrange("p t b -> p (t b)").bitcast(I32))
         for q in range(QUADS):
             nc.gpsimd.dma_start(
@@ -78,13 +78,12 @@ def tile_list_tgn_gruP_kernel(
                 w_scales_dram[g][0, 4 * q : 4 * q + 4, :].bitcast(I32),
             )
 
-        for g in (R, Z):
-            for q in range(QUADS):
-                load_w_scales(nc.gpsimd, g, q)
-        windows = [keep.tile([P, T], F32, name="window%d" % w) for w in range(WINDOWS)]
+        for g in (R, C, Z):
+            nc.gpsimd.dma_start(bias_rows[TILES * g : TILES * (g + 1), :], b_dram[g].rearrange("(i p) -> i p", p=P))
+        for q in range(QUADS):
+            load_w_scales(nc.gpsimd, Z, q)
+        windows = [keep.tile([P, T], F32, name="window0")]
         nc.vector.memset(windows[0][:], 0.0)
-        nc.vector.memset(windows[1][:], 0.0)
-        nc.vector.memset(windows[2][:], 0.0)
 
         x_raw = {}
 
@@ -121,13 +120,10 @@ def tile_list_tgn_gruP_kernel(
         def load_state(i):
             nc.sync.dma_start(state[i % 3][:], hT[P * i : P * (i + 1), :])
 
-        def load_bias(g):
-            nc.sync.dma_start(bias_rows[TILES * g : TILES * (g + 1), :], b_dram[g].rearrange("(i p) -> i p", p=P))
-
-        weight = [keep.tile([P, HALF], F32, name="weight%d" % h) for h in range(HALVES)]
+        weight = keep.tile([P, J], F32, name="weight")
 
         def load_weight(h):
-            nc.sync.dma_start(weight[h][:], wgo[:, h * HALF : (h + 1) * HALF])
+            nc.sync.dma_start(weight[:, h * HALF : (h + 1) * HALF], wgo[:, h * HALF : (h + 1) * HALF])
 
         load_x(0)
         load_u(0, 0)
@@ -135,14 +131,15 @@ def tile_list_tgn_gruP_kernel(
         load_w(R, 0)
         load_u(0, 2)
         load_u(0, 3)
-        load_bias(R)
+        load_w_scales(nc.sync, R, 0)
         load_w(C, 0)
-        load_bias(C)
+        load_w_scales(nc.sync, R, 1)
         load_state(0)
-        load_bias(Z)
+        load_w_scales(nc.sync, R, 2)
+        load_w_scales(nc.sync, R, 3)
         load_u(0, 4)
-        load_w_scales(nc.sync, C, 0)
         load_u(0, 5)
+        load_w_scales(nc.sync, C, 0)
         load_w_scales(nc.sync, C, 1)
         load_w_scales(nc.sync, C, 2)
         load_x(1)
@@ -230,7 +227,10 @@ def tile_list_tgn_gruP_kernel(
         def turn_biases():
             bank = psum.tile([P, 4, P], F32, name="turned", tag="turned", bufs=2)
             nc.tensor.transpose(bank[:, 0, :], bias_rows[:], ident[:])
-            nc.scalar.copy(bias[:], bank[:, 0, 0 : 3 * TILES])
+            nc.scalar.copy(bias[:, 0 : 2 * TILES], bank[:, 0, 0 : 2 * TILES])
+            nc.scalar.activation(
+                out=bias[:, 2 * TILES :], in_=bank[:, 0, 2 * TILES : 3 * TILES], func=ACT.Copy, scale=-1.0
+            )
 
         def x_pass(bank, g, i, h, stop):
             part = min(i // 2, 2)
@@ -256,95 +256,90 @@ def tile_list_tgn_gruP_kernel(
                     start=(start and a == 0), stop=(a == PASSES - 1),
                 )
 
-        DEPTH = 5
-        Z_DEPTH = 4
-        work = [keep.tile([P, 2 * HALF], F32, name="work%d" % k) for k in range(DEPTH)]
-        z_tiles = [keep.tile([P, HALF], F32, name="z%d" % k) for k in range(Z_DEPTH)]
+        work = [keep.tile([P, J], F32, name="work%d" % k) for k in range(3)]
+        r_tile = keep.tile([P, J], F32, name="r")
+        keep_tiles = [keep.tile([P, J], F32, name="keep%d" % k) for k in range(2)]
 
-        def r_of(s):
-            return work[s % DEPTH][:, HALF // 2 : HALF // 2 + HALF]
+        def cols(h):
+            return slice(0, J) if h is None else slice(h * HALF, (h + 1) * HALF)
 
-        def old_of(s):
-            return work[s % DEPTH][:, 0:HALF]
+        def list_of(h):
+            return offsets[:] if h is None else offs_of(h)
 
-        def new_of(s):
-            if s == 0:
-                return z_of(3)
-            return value_of(s + 3)
-
-        def value_of(s):
-            return work[(s - 1) % DEPTH][:, HALF : 2 * HALF]
-
-        def z_of(s):
-            return z_tiles[s % Z_DEPTH][:]
-
-        def gate(g, s, dst):
-            i, h = divmod(s, HALVES)
+        def gate(g, i, h):
             bank = psum.tile([P, HALF], F32, name="gate_sum", tag="gate_sum%d" % g)
             x_pass(bank, g, i, h, False)
             v_passes(bank, g, i, h, False)
+            dst = r_tile if g == R else keep_tiles[i % 2]
             nc.scalar.activation(
-                out=dst, in_=bank[:], func=ACT.Sigmoid, bias=bias[:, TILES * g + i : TILES * g + i + 1]
+                out=dst[:, cols(h)], in_=bank[:], func=ACT.Sigmoid,
+                bias=bias[:, TILES * g + i : TILES * g + i + 1], scale=(1.0 if g == R else -1.0),
             )
 
-        def front(s):
-            i, h = divmod(s, HALVES)
-            y = value_of(s)
+        def reset(i, h):
             hn = psum.tile([P, HALF], F32, name="hn", tag="hn")
             v_passes(hn, C, i, h, True)
+            nc.vector.tensor_tensor(work[i % 3][:, cols(h)], hn[:], r_tile[:, cols(h)], ALU.mult)
+
+        def add_message(i, h):
             xn = psum.tile([P, HALF], F32, name="xn", tag="xn")
             x_pass(xn, C, i, h, True)
-            nc.vector.tensor_tensor(y, hn[:], r_of(s), ALU.mult)
-            nc.vector.tensor_copy(old_of(s), state[i % 3][:].indirect(offs_of(h)))
-            nc.vector.tensor_tensor(y, xn[:], y, ALU.add)
+            pre = work[i % 3][:, cols(h)]
+            nc.vector.tensor_tensor(pre, xn[:], pre, ALU.add)
 
-        def candidate(s):
-            i = s // HALVES
-            nc.scalar.activation(
-                out=value_of(s), in_=value_of(s), func=ACT.Tanh, bias=bias[:, TILES * C + i : TILES * C + i + 1]
+        def candidate(i, h):
+            pre = work[i % 3][:, cols(h)]
+            nc.scalar.activation(out=pre, in_=pre, func=ACT.Tanh, bias=bias[:, TILES * C + i : TILES * C + i + 1])
+
+        def difference(i, h=None):
+            nc.vector.tensor_tensor(
+                work[(i - 1) % 3][:, cols(h)], state[i % 3][:].indirect(list_of(h)), work[i % 3][:, cols(h)], ALU.subtract
             )
 
-        def blend(s):
-            y = value_of(s)
-            old = old_of(s)
-            nc.gpsimd.tensor_tensor(y, y, old, ALU.subtract)
-            nc.gpsimd.tensor_tensor(y, y, z_of(s), ALU.mult)
-            nc.gpsimd.tensor_tensor(y, y, old, ALU.add)
+        def damp(i, h=None):
+            y = work[(i - 1) % 3][:, cols(h)]
+            nc.vector.tensor_tensor(y, y, keep_tiles[i % 2][:, cols(h)], ALU.mult)
 
-        def weigh(s):
-            nc.gpsimd.tensor_tensor(new_of(s), value_of(s), weight[s % HALVES][:], ALU.mult)
+        def blend(i, h=None):
+            y = work[(i - 1) % 3][:, cols(h)]
+            nc.vector.tensor_tensor(y, y, work[i % 3][:, cols(h)], ALU.add)
 
-        def scatter(s):
-            i, h = divmod(s, HALVES)
+        def scatter(i, h=None):
             window = windows[i % WINDOWS]
-            nc.vector.tensor_copy(window[:].indirect(offs_of(h)), new_of(s))
-            if h == HALVES - 1:
-                nc.sync.dma_start(out_0[P * i : P * (i + 1), :], window[:])
+            nc.vector.tensor_tensor(
+                window[:].indirect(list_of(h)), work[(i - 1) % 3][:, cols(h)], weight[:, cols(h)], ALU.mult
+            )
+
+        def store(i):
+            nc.sync.dma_start(out_0[P * i : P * (i + 1), :], windows[i % WINDOWS][:])
 
         y_scales = keep.tile([P, TILES, T // QUADS], U8, name="y_scales", align_bytes=64)
 
         grouped, backs = {}, {}
 
-        def turn(i, half, tags, copies, place=None):
+        turned = {}
+
+        def bank_tile(shape, tag):
+            return psum.tile(shape, F32, name=tag, tag=tag, bufs=(2 if tag in ("turned", "back") else 1))
+
+        def turn(i, grp, tag="turned"):
             window = windows[i % WINDOWS]
-            backs[i, half] = psum.tile([P, 2, 2, P], F32, name="back", tag="back", bufs=2)
-            for k in range(2):
-                grp = 2 * half + k
-                turned = psum.tile([P, QUADS, P], F32, name="turned", tag=tags[k], bufs=(2 if tags[k] == "turned" else 1))
-                for q in range(QUADS):
-                    t0 = (T // QUADS) * q + P * grp
-                    nc.tensor.transpose(turned[:, q, :], window[:, t0 : t0 + P], ident[:])
-                if place is None:
-                    pairs_tile = ring.tile([P, 2 * P], F32, name="pairs", tag="pairs", bufs=4)
-                    pairs = pairs_tile[:]
-                else:
-                    pairs = place[:, 2 * P * k : 2 * P * (k + 1)]
-                copies[k](
-                    pairs.bitcast(BF16).rearrange("p (u m e) -> p u m e", u=2, e=2),
-                    turned[:].rearrange("p q (m u e) -> p u (q m) e", u=2, e=2),
-                )
-                for u in range(2):
-                    nc.tensor.transpose(backs[i, half][:, k, u, :], pairs[:, P * u : P * (u + 1)], ident[:])
+            turned[i, grp] = bank_tile([P, QUADS, P], tag)
+            for q in range(QUADS):
+                t0 = (T // QUADS) * q + P * grp
+                nc.tensor.transpose(turned[i, grp][:, q, :], window[:, t0 : t0 + P], ident[:])
+
+        def pack(i, grp, copy, tag="back"):
+            half, k = divmod(grp, 2)
+            if k == 0:
+                backs[i, half] = bank_tile([P, 2, 2, P], tag)
+            pairs = ring.tile([P, 2 * P], F32, name="pairs", tag="pairs", bufs=4)
+            copy(
+                pairs[:].bitcast(BF16).rearrange("p (u m e) -> p u m e", u=2, e=2),
+                turned[i, grp][:].rearrange("p q (m u e) -> p u (q m) e", u=2, e=2),
+            )
+            for u in range(2):
+                nc.tensor.transpose(backs[i, half][:, k, u, :], pairs[:, P * u : P * (u + 1)], ident[:])
 
         def group(i, half, copy):
             if half == 0:
@@ -366,66 +361,105 @@ def tile_list_tgn_gruP_kernel(
                     y_codes[32 * q : 32 * (q + 1), :].bitcast(I32),
                 )
 
+        on_scalar, on_vector = nc.scalar.copy, nc.vector.tensor_copy
         gather_table(0)
         quantize_x(0)
         turn_biases()
-        scalar_only = [nc.scalar.copy, nc.scalar.copy]
         for piece in range(4):
             round_u(0, piece)
-        gate(R, 0, r_of(0))
-        front(0)
-        candidate(0)
+        gate(R, 0, 0)
+        reset(0, 0)
+        add_message(0, 0)
+        candidate(0, 0)
         round_u(0, 4)
         round_u(0, 5)
-        gate(Z, 0, z_of(0))
-        blend(0)
-        weigh(0)
+        gate(Z, 0, 0)
         gather_table(1)
+        second_window = keep.tile([P, T], F32, name="window1", tag="second_window")
+        windows.append(second_window)
+        nc.vector.memset(second_window[:], 0.0)
         quantize_x(1)
-        gate(R, 1, r_of(1))
-        front(1)
-        gate(Z, 1, z_of(1))
+        difference(0, 0)
+        damp(0, 0)
+        blend(0, 0)
+        scatter(0, 0)
+        gate(R, 0, 1)
+        reset(0, 1)
+        add_message(0, 1)
+        candidate(0, 1)
+        gate(Z, 0, 1)
+        for piece in range(6):
+            round_u(1, piece)
+        difference(0, 1)
+        damp(0, 1)
+        blend(0, 1)
+        for h in range(HALVES):
+            gate(R, 1, h)
+            reset(1, h)
+            add_message(1, h)
+            gate(Z, 1, h)
+        for piece in range(6):
+            round_u(2, piece)
+        load_state(3)
 
-        def round_piece(k, j):
-            i, piece = divmod(3 * (k + 7) + j, 3 * PASSES)
-            if i < TILES:
-                round_u(i, piece)
-
-        for k in range(-5, STEPS + 1):
-            if 0 <= k < STEPS:
-                scatter(k)
-            if 2 <= k + 3 < STEPS:
-                front(k + 3)
-            if 1 <= k + 1 < STEPS - 1:
-                weigh(k + 1)
-            if k % 2 == 0 and k >= -2 and k // 2 + 4 < TILES:
-                load_state(k // 2 + 4)
-            if 0 <= k - 3 < STEPS - 2:
-                group((k - 3) // 2, (k - 3) % 2, nc.scalar.copy)
-                if (k - 3) % 2 == 1:
-                    planes((k - 3) // 2)
-            round_piece(k, 0)
-            if 1 <= k + 2 < STEPS:
-                candidate(k + 2)
-                blend(k + 2)
-            if 2 <= k + 3 < STEPS:
-                gate(Z, k + 3, z_of(k + 3))
-            if 2 <= k + 4 < STEPS:
-                gate(R, k + 4, r_of(k + 4))
-            if 0 <= k - 2 < STEPS - 4:
-                turn((k - 2) // 2, (k - 2) % 2, ("turned", "turned"), scalar_only)
-            if k == STEPS - 3:
-                turn(TILES - 2, 0, ("turned", "turned"), scalar_only)
-                turn(TILES - 2, 1, ("turned", "turned"), scalar_only, new_of(STEPS - 1))
-                weigh(STEPS - 1)
-            round_piece(k, 1)
-            round_piece(k, 2)
-        both = [nc.scalar.copy, nc.vector.tensor_copy]
-        turn(TILES - 1, 0, ("turned", "turned"), both)
-        turn(TILES - 1, 1, ("hn", "xn"), both)
-        group(TILES - 1, 0, nc.scalar.copy)
-        group(TILES - 1, 1, nc.vector.tensor_copy)
-        planes(TILES - 1)
+        for i in range(TILES):
+            ahead, nxt, done, coming = i + 2, i + 1, i - 1, i + 3
+            scatter(i, 1 if i == 0 else None)
+            store(i)
+            if nxt < TILES:
+                candidate(nxt, 0)
+                candidate(nxt, 1)
+                difference(nxt)
+                if nxt + 3 < TILES:
+                    load_state(nxt + 3)
+            if ahead < TILES:
+                gate(R, ahead, 0)
+                reset(ahead, 0)
+            if nxt < TILES:
+                damp(nxt)
+            if ahead < TILES:
+                gate(Z, ahead, 0)
+                add_message(ahead, 0)
+                gate(R, ahead, 1)
+                reset(ahead, 1)
+            if nxt < TILES:
+                blend(nxt)
+            if ahead < TILES:
+                add_message(ahead, 1)
+            if coming < TILES:
+                round_u(coming, 0)
+            if ahead < TILES:
+                gate(Z, ahead, 1)
+            if coming < TILES:
+                for piece in range(1, 5):
+                    round_u(coming, piece)
+            if done >= 0:
+                turn(done, 0)
+                turn(done, 1)
+                pack(done, 0, on_scalar)
+                turn(done, 2)
+                pack(done, 1, on_scalar)
+                turn(done, 3)
+            if coming < TILES:
+                round_u(coming, 5)
+            if done >= 0:
+                pack(done, 2, on_scalar)
+                pack(done, 3, on_scalar)
+                group(done, 0, on_scalar)
+                group(done, 1, on_scalar)
+                planes(done)
+        last = TILES - 1
+        turn(last, 0)
+        turn(last, 1)
+        turn(last, 2, "back")
+        turn(last, 3, "back")
+        pack(last, 0, on_scalar, "hn")
+        pack(last, 1, on_vector)
+        pack(last, 2, on_scalar, "xn")
+        pack(last, 3, on_vector)
+        group(last, 0, on_scalar)
+        group(last, 1, on_vector)
+        planes(last)
         scales_dram = out_2.rearrange("a (i r) t -> r (a i) t", r=4)
         for q in range(QUADS):
             nc.scalar.dma_start(

@@ -19,15 +19,26 @@ ALU = mybir.AluOpType
 
 P = 128
 PACK = 4
+K_PASS = P * PACK
+PASSES = M // K_PASS
 HALF = 512
 HALVES = J // HALF
 TILES = N // P
-STEPS = TILES * HALVES
-PASSES = M // 512
+LAST = TILES - 1
 QUADS = 4
-CHUNKS = [(0, 128), (128, 128), (256, 256), (512, 256), (768, 256)]
-WINDOWS = 2
+QUAD_ROWS = P // QUADS
+SPAN = T // QUADS
+GROUPS = SPAN // P
+
 R, C, Z = 0, 1, 2
+PIECES = 3 * PASSES
+U_COLS = PASSES * P
+
+U_CHUNKS = [(0, 128), (128, 128), (256, 256), (512, 256), (768, 256)]
+SLOT = 256
+W_PARTS = [(0, 256), (256, 256), (512, 512)]
+WINDOWS = 3
+STATES = 3
 
 
 def tile_list_tgn_gruP_kernel(
@@ -39,42 +50,46 @@ def tile_list_tgn_gruP_kernel(
     w_scales_dram = [wr_scales, wn_scales, wz_scales]
     u_dram = [ur, un, uz]
     b_dram = [br, bn, bz]
+    on_scalar, on_vector = nc.scalar.copy, nc.vector.tensor_copy
 
     with ExitStack() as ctx:
-        keep = ctx.enter_context(tc.tile_pool(name="keep", bufs=1))
+        held = ctx.enter_context(tc.tile_pool(name="held", bufs=1))
         ring = ctx.enter_context(tc.tile_pool(name="ring", bufs=2))
         psum = ctx.enter_context(tc.psum_pool(name="psum", bufs=1))
 
-        offsets = keep.tile([P, J // 16], U16, name="offsets")
+        offsets = held.tile([P, J // 16], U16, name="offsets")
         nc.sync.dma_start(offsets[:], offs)
 
-        def offs_of(h):
-            return offsets[:, h * (HALF // 16) : (h + 1) * (HALF // 16)]
+        def events(h):
+            return slice(0, J) if h is None else slice(h * HALF, (h + 1) * HALF)
 
-        table_scales = keep.tile([P, PASSES, T], U8, name="table_scales", align_bytes=64)
+        def list_of(h):
+            return offsets[:] if h is None else offsets[:, h * (HALF // 16) : (h + 1) * (HALF // 16)]
+
+        def bank_tile(shape, tag):
+            return psum.tile(shape, F32, name=tag, tag=tag, bufs=(2 if tag in ("turned", "back") else 1))
+
+        table_scales = held.tile([P, PASSES, T], U8, name="table_scales", align_bytes=64)
         nc.vector.memset(table_scales[:].rearrange("p a t -> p (a t)").bitcast(I32), 0)
-        w_scales = [keep.tile([P, N], U8, name="w_scales%d" % g, align_bytes=64) for g in (R, C, Z)]
+        w_scales = [held.tile([P, N], U8, name="w_scales%d" % g, align_bytes=64) for g in (R, C, Z)]
         for g in (R, C, Z):
             nc.vector.memset(w_scales[g][:].bitcast(I32), 0)
-        bias_rows = keep.tile([P, P], F32, name="bias_rows")
+        bias_rows = held.tile([P, P], F32, name="bias_rows")
         nc.vector.memset(bias_rows[:], 0.0)
-        warm = keep.tile([P, 16], F32, name="warm")
-        nc.vector.memset(warm[:, 0:8], 0.0)
-        nc.scalar.activation(out=warm[:, 8:16], in_=warm[:, 0:8], func=ACT.Sigmoid)
 
-        table_words = keep.tile([P, T], U32, name="table_words", tag="second_window")
+        table_words = held.tile([P, T], U32, name="table_words", tag="second_window")
         nc.sync.dma_start(table_words[:].bitcast(I32), tab_words[0].rearrange("p t b -> p (t b)").bitcast(I32))
         for q in range(QUADS):
             nc.gpsimd.dma_start(
-                table_scales[32 * q : 32 * q + 4, :, :].bitcast(I32),
+                table_scales[QUAD_ROWS * q : QUAD_ROWS * q + 4, :, :].bitcast(I32),
                 tab_scales[:, 4 * q : 4 * q + 4, :].rearrange("a r t -> r a t").bitcast(I32),
             )
-        ident = keep.tile([P, P], F32, name="ident")
+        ident = held.tile([P, P], F32, name="ident")
         make_identity(nc, ident[:])
 
         def load_w_scales(queue, g, q):
             queue.dma_start(
-                w_scales[g][32 * q : 32 * q + 4, :].bitcast(I32),
+                w_scales[g][QUAD_ROWS * q : QUAD_ROWS * q + 4, :].bitcast(I32),
                 w_scales_dram[g][0, 4 * q : 4 * q + 4, :].bitcast(I32),
             )
 
@@ -82,48 +97,57 @@ def tile_list_tgn_gruP_kernel(
             nc.gpsimd.dma_start(bias_rows[TILES * g : TILES * (g + 1), :], b_dram[g].rearrange("(i p) -> i p", p=P))
         for q in range(QUADS):
             load_w_scales(nc.gpsimd, Z, q)
-        windows = [keep.tile([P, T], F32, name="window0")]
-        nc.vector.memset(windows[0][:], 0.0)
+
+        windows = []
+
+        def open_window(tag):
+            window = held.tile([P, T], F32, name="window%d" % len(windows), tag=tag)
+            windows.append(window)
+            return window
+
+        nc.vector.memset(open_window("first_window")[:], 0.0)
 
         x_raw = {}
 
         def load_x(h):
-            x_raw[h] = keep.tile([P, PACK, HALF], F32, name="x_raw%d" % h)
-            nc.sync.dma_start(x_raw[h][:], x[:, h * HALF : (h + 1) * HALF].rearrange("(p t) j -> p t j", t=PACK))
+            x_raw[h] = held.tile([P, PACK, HALF], F32, name="x_raw%d" % h, tag=("x_raw", "third_window")[h])
+            nc.sync.dma_start(x_raw[h][:], x[:, events(h)].rearrange("(p t) j -> p t j", t=PACK))
 
-        u_slots = [[keep.tile([P, PACK * 256], F32, name="u_raw%d_%d" % (k, piece)) for piece in range(6)] for k in range(2)]
+        u_slots = [
+            [held.tile([P, PACK * SLOT], F32, name="u_raw%d_%d" % (k, piece)) for piece in range(PIECES)]
+            for k in range(2)
+        ]
 
         def u_raw(c, piece):
-            n0, width = CHUNKS[c]
-            e0 = PACK * (n0 % 256)
-            return u_slots[(n0 // 256) % 2][piece][:, e0 : e0 + PACK * width].rearrange("p (t n) -> p t n", t=PACK)
+            n0, width = U_CHUNKS[c]
+            e0 = PACK * (n0 % SLOT)
+            return u_slots[(n0 // SLOT) % 2][piece][:, e0 : e0 + PACK * width].rearrange("p (t n) -> p t n", t=PACK)
 
         def load_u(c, piece):
-            n0, width = CHUNKS[c]
+            n0, width = U_CHUNKS[c]
             g, a = divmod(piece, PASSES)
             nc.sync.dma_start(
                 u_raw(c, piece),
-                u_dram[g][512 * a : 512 * (a + 1), n0 : n0 + width].rearrange("(p t) n -> p t n", t=PACK),
+                u_dram[g][K_PASS * a : K_PASS * (a + 1), n0 : n0 + width].rearrange("(p t) n -> p t n", t=PACK),
             )
 
         w_words = {}
-        W_PARTS = [(0, 256), (256, 256), (512, 512)]
 
         def load_w(g, part):
             c0, width = W_PARTS[part]
-            w_words[g, part] = keep.tile([P, width], U32, name="w_words%d_%d" % (g, part), align_bytes=64)
+            w_words[g, part] = held.tile([P, width], U32, name="w_words%d_%d" % (g, part), align_bytes=64)
             flat = w_words_dram[g][0].rearrange("p n b -> p (n b)")
-            nc.sync.dma_start(w_words[g, part][:].bitcast(I32), flat[:, 4 * c0 : 4 * (c0 + width)].bitcast(I32))
+            nc.sync.dma_start(w_words[g, part][:].bitcast(I32), flat[:, PACK * c0 : PACK * (c0 + width)].bitcast(I32))
 
-        state = [keep.tile([P, T], F32, name="state%d" % k) for k in range(3)]
+        state = [held.tile([P, T], F32, name="state%d" % k) for k in range(STATES)]
 
         def load_state(i):
-            nc.sync.dma_start(state[i % 3][:], hT[P * i : P * (i + 1), :])
+            nc.sync.dma_start(state[i % STATES][:], hT[P * i : P * (i + 1), :])
 
-        weight = keep.tile([P, J], F32, name="weight")
+        weight = held.tile([P, J], F32, name="weight")
 
         def load_weight(h):
-            nc.sync.dma_start(weight[:, h * HALF : (h + 1) * HALF], wgo[:, h * HALF : (h + 1) * HALF])
+            nc.sync.dma_start(weight[:, events(h)], wgo[:, events(h)])
 
         load_x(0)
         load_u(0, 0)
@@ -146,15 +170,15 @@ def tile_list_tgn_gruP_kernel(
         load_w_scales(nc.sync, C, 3)
         load_w(Z, 0)
         load_weight(0)
-        for piece in range(4):
+        for piece in range(PASSES * Z):
             load_u(1, piece)
         load_state(1)
         load_weight(1)
-        load_u(1, 4)
-        load_u(1, 5)
+        for piece in range(PASSES * Z, PIECES):
+            load_u(1, piece)
         for g in (R, C, Z):
-            load_u(2, 2 * g)
-            load_u(2, 2 * g + 1)
+            for a in range(PASSES):
+                load_u(2, PASSES * g + a)
             load_w(g, 1)
             if g == C:
                 load_state(2)
@@ -162,52 +186,55 @@ def tile_list_tgn_gruP_kernel(
         v_codes, v_scales, x_codes, x_scales = {}, {}, {}, {}
 
         def gather_table(h):
-            picked = keep.tile([P, HALF], U32, name="picked%d" % h)
-            nc.vector.tensor_copy(picked[:], table_words[:].indirect(offs_of(h)))
-            v_codes[h] = keep.tile([P, PASSES, 2 * HALF], U8, name="v_codes%d" % h, align_bytes=64)
+            picked = held.tile([P, HALF], U32, name="picked%d" % h)
+            nc.vector.tensor_copy(picked[:], table_words[:].indirect(list_of(h)))
+            v_codes[h] = held.tile([P, PASSES, 2 * HALF], U8, name="v_codes%d" % h, align_bytes=64)
             nc.vector.tensor_copy(
                 v_codes[h][:].bitcast(U16),
                 picked[:].bitcast(U16).rearrange("p (j d) -> p d j", d=PASSES),
             )
             for a in range(PASSES):
-                v_scales[h, a] = keep.tile([P, HALF], U8, name="v_scales%d_%d" % (h, a), align_bytes=64)
-                nc.vector.tensor_copy(v_scales[h, a][:], table_scales[:, a, :].indirect(offs_of(h)))
+                v_scales[h, a] = held.tile([P, HALF], U8, name="v_scales%d_%d" % (h, a), align_bytes=64)
+                nc.vector.tensor_copy(v_scales[h, a][:], table_scales[:, a, :].indirect(list_of(h)))
 
-        def interleave(copy, dst, raw):
-            copy(
+        def interleave(dst, raw):
+            nc.scalar.copy(
                 dst.rearrange("p (c i) t -> p c t i", i=4),
                 raw.rearrange("p t (c i) -> p c t i", i=4),
             )
 
         def quantize_x(h):
             x_bf = ring.tile([P, HALF, PACK], BF16, name="x_bf", tag="x_bf", bufs=1, align_bytes=64)
-            interleave(nc.scalar.copy, x_bf[:], x_raw[h][:])
-            x_codes[h] = keep.tile([P, HALF], U32, name="x_codes%d" % h, align_bytes=64)
-            x_scales[h] = keep.tile([P, HALF], U8, name="x_scales%d" % h, align_bytes=64)
+            interleave(x_bf[:], x_raw[h][:])
+            x_codes[h] = held.tile([P, HALF], U32, name="x_codes%d" % h, align_bytes=64)
+            x_scales[h] = held.tile([P, HALF], U8, name="x_scales%d" % h, align_bytes=64)
             nc.vector.quantize_mx(
                 out=x_codes[h][:].bitcast(FP8X4), scales=x_scales[h][:],
                 in_=x_bf[:].rearrange("p j t -> p (j t)"),
             )
 
-        UW = PASSES * P
-        u_bf = [keep.tile([P, 3 * UW * PACK], BF16, name="u_bf%d" % k, align_bytes=64) for k in range(2)]
-        u_codes = [keep.tile([P, 3 * UW], U32, name="u_codes%d" % k, align_bytes=64) for k in range(2)]
-        u_scales = [keep.tile([P, 3 * UW], U8, name="u_scales%d" % k, align_bytes=64) for k in range(2)]
+        u_bf = [held.tile([P, 3 * U_COLS * PACK], BF16, name="u_bf%d" % k, align_bytes=64) for k in range(2)]
+        u_codes = [held.tile([P, 3 * U_COLS], U32, name="u_codes%d" % k, align_bytes=64) for k in range(2)]
+        u_scales = [held.tile([P, 3 * U_COLS], U8, name="u_scales%d" % k, align_bytes=64) for k in range(2)]
 
-        def chunk_of(i):
-            for c, (n0, width) in enumerate(CHUNKS):
-                if n0 <= P * i < n0 + width:
-                    return c, P * i - n0
+        def quantize_u(i, g0, g1):
+            nc.vector.quantize_mx(
+                out=u_codes[i % 2][:, g0 * U_COLS : g1 * U_COLS].bitcast(FP8X4),
+                scales=u_scales[i % 2][:, g0 * U_COLS : g1 * U_COLS],
+                in_=u_bf[i % 2][:, g0 * U_COLS * PACK : g1 * U_COLS * PACK],
+            )
 
         def round_u(i, piece):
             g, a = divmod(piece, PASSES)
-            c, off = chunk_of(i)
-            c0 = (g * UW + a * P) * PACK
+            c = max(k for k, (n0, width) in enumerate(U_CHUNKS) if n0 <= P * i)
+            n_off = P * i - U_CHUNKS[c][0]
+            c0 = piece * P * PACK
             dst = u_bf[i % 2][:, c0 : c0 + P * PACK].rearrange("p (n t) -> p n t", t=PACK)
-            interleave(nc.scalar.copy, dst, u_raw(c, piece)[:, :, off : off + P])
-            if i in (1, 3):
+            interleave(dst, u_raw(c, piece)[:, :, n_off : n_off + P])
+            slot_is_empty = (P * (i + 1)) % SLOT == 0
+            if slot_is_empty and c + 2 < len(U_CHUNKS):
                 load_u(c + 2, piece)
-                if i == 1 and a == 1:
+                if i == 1 and a == PASSES - 1:
                     load_w(g, 2)
             if a == PASSES - 1:
                 if i == 0 or g == Z:
@@ -215,25 +242,19 @@ def tile_list_tgn_gruP_kernel(
                 elif g == C:
                     quantize_u(i, R, Z)
 
-        def quantize_u(i, g0, g1):
-            nc.vector.quantize_mx(
-                out=u_codes[i % 2][:, g0 * UW : g1 * UW].bitcast(FP8X4),
-                scales=u_scales[i % 2][:, g0 * UW : g1 * UW],
-                in_=u_bf[i % 2][:, g0 * UW * PACK : g1 * UW * PACK],
-            )
-
-        bias = keep.tile([P, 3 * TILES], F32, name="bias")
+        bias = held.tile([P, 3 * TILES], F32, name="bias")
 
         def turn_biases():
-            bank = psum.tile([P, 4, P], F32, name="turned", tag="turned", bufs=2)
+            bank = bank_tile([P, QUADS, P], "turned")
             nc.tensor.transpose(bank[:, 0, :], bias_rows[:], ident[:])
-            nc.scalar.copy(bias[:, 0 : 2 * TILES], bank[:, 0, 0 : 2 * TILES])
-            nc.scalar.activation(
-                out=bias[:, 2 * TILES :], in_=bank[:, 0, 2 * TILES : 3 * TILES], func=ACT.Copy, scale=-1.0
-            )
+            nc.scalar.copy(bias[:, 0 : Z * TILES], bank[:, 0, 0 : Z * TILES])
+            nc.vector.tensor_scalar_mul(bias[:, Z * TILES :], bank[:, 0, Z * TILES : 3 * TILES], -1.0)
+
+        def bias_of(g, i):
+            return bias[:, TILES * g + i : TILES * g + i + 1]
 
         def x_pass(bank, g, i, h, stop):
-            part = min(i // 2, 2)
+            part = max(k for k, (n0, width) in enumerate(W_PARTS) if n0 <= P * i)
             c0 = P * i - W_PARTS[part][0]
             nc.tensor.matmul_mx(
                 out=bank[:],
@@ -244,9 +265,9 @@ def tile_list_tgn_gruP_kernel(
                 start=True, stop=stop,
             )
 
-        def v_passes(bank, g, i, h, start):
+        def table_passes(bank, g, i, h, start):
             for a in range(PASSES):
-                cols = slice(g * UW + a * P, g * UW + (a + 1) * P)
+                cols = slice(g * U_COLS + a * P, g * U_COLS + (a + 1) * P)
                 nc.tensor.matmul_mx(
                     out=bank[:],
                     lhsT=u_codes[i % 2][:, cols].bitcast(FP8X4),
@@ -256,213 +277,222 @@ def tile_list_tgn_gruP_kernel(
                     start=(start and a == 0), stop=(a == PASSES - 1),
                 )
 
-        work = [keep.tile([P, J], F32, name="work%d" % k) for k in range(3)]
-        r_tile = keep.tile([P, J], F32, name="r")
-        keep_tiles = [keep.tile([P, J], F32, name="keep%d" % k) for k in range(2)]
-
-        def cols(h):
-            return slice(0, J) if h is None else slice(h * HALF, (h + 1) * HALF)
-
-        def list_of(h):
-            return offsets[:] if h is None else offs_of(h)
+        cand = [held.tile([P, J], F32, name="cand%d" % k) for k in range(2)]
+        mix = held.tile([P, J], F32, name="mix")
+        reset = held.tile([P, J], F32, name="reset", align_bytes=64)
+        keep = [held.tile([P, J], F32, name="keep%d" % k) for k in range(2)]
 
         def gate(g, i, h):
-            bank = psum.tile([P, HALF], F32, name="gate_sum", tag="gate_sum%d" % g)
+            bank = bank_tile([P, HALF], "gate_sum%d" % g)
             x_pass(bank, g, i, h, False)
-            v_passes(bank, g, i, h, False)
-            dst = r_tile if g == R else keep_tiles[i % 2]
+            table_passes(bank, g, i, h, False)
+            dst = reset if g == R else keep[i % 2]
             nc.scalar.activation(
-                out=dst[:, cols(h)], in_=bank[:], func=ACT.Sigmoid,
-                bias=bias[:, TILES * g + i : TILES * g + i + 1], scale=(1.0 if g == R else -1.0),
+                out=dst[:, events(h)], in_=bank[:], func=ACT.Sigmoid,
+                bias=bias_of(g, i), scale=(1.0 if g == R else -1.0),
             )
 
-        def reset(i, h):
-            hn = psum.tile([P, HALF], F32, name="hn", tag="hn")
-            v_passes(hn, C, i, h, True)
-            nc.vector.tensor_tensor(work[i % 3][:, cols(h)], hn[:], r_tile[:, cols(h)], ALU.mult)
+        def apply_reset(i, h):
+            hn = bank_tile([P, HALF], "hn")
+            table_passes(hn, C, i, h, True)
+            nc.vector.tensor_tensor(cand[i % 2][:, events(h)], hn[:], reset[:, events(h)], ALU.mult)
 
         def add_message(i, h):
-            xn = psum.tile([P, HALF], F32, name="xn", tag="xn")
+            xn = bank_tile([P, HALF], "xn")
             x_pass(xn, C, i, h, True)
-            pre = work[i % 3][:, cols(h)]
-            nc.vector.tensor_tensor(pre, xn[:], pre, ALU.add)
+            total = cand[i % 2][:, events(h)]
+            nc.vector.tensor_tensor(total, xn[:], total, ALU.add)
 
         def candidate(i, h):
-            pre = work[i % 3][:, cols(h)]
-            nc.scalar.activation(out=pre, in_=pre, func=ACT.Tanh, bias=bias[:, TILES * C + i : TILES * C + i + 1])
+            total = cand[i % 2][:, events(h)]
+            nc.scalar.activation(out=total, in_=total, func=ACT.Tanh, bias=bias_of(C, i))
 
-        def difference(i, h=None):
+        def difference(i, h):
             nc.vector.tensor_tensor(
-                work[(i - 1) % 3][:, cols(h)], state[i % 3][:].indirect(list_of(h)), work[i % 3][:, cols(h)], ALU.subtract
+                mix[:, events(h)], state[i % STATES][:].indirect(list_of(h)), cand[i % 2][:, events(h)], ALU.subtract
             )
 
-        def damp(i, h=None):
-            y = work[(i - 1) % 3][:, cols(h)]
-            nc.vector.tensor_tensor(y, y, keep_tiles[i % 2][:, cols(h)], ALU.mult)
+        def damp(i, h):
+            nc.vector.tensor_tensor(mix[:, events(h)], mix[:, events(h)], keep[i % 2][:, events(h)], ALU.mult)
 
-        def blend(i, h=None):
-            y = work[(i - 1) % 3][:, cols(h)]
-            nc.vector.tensor_tensor(y, y, work[i % 3][:, cols(h)], ALU.add)
+        def blend(i, h, dst):
+            nc.vector.tensor_tensor(dst, mix[:, events(h)], cand[i % 2][:, events(h)], ALU.add)
 
-        def scatter(i, h=None):
-            window = windows[i % WINDOWS]
-            nc.vector.tensor_tensor(
-                window[:].indirect(list_of(h)), work[(i - 1) % 3][:, cols(h)], weight[:, cols(h)], ALU.mult
-            )
+        def scatter(i, h, src):
+            nc.vector.tensor_tensor(windows[i % WINDOWS][:].indirect(list_of(h)), src, weight[:, events(h)], ALU.mult)
 
         def store(i):
             nc.sync.dma_start(out_0[P * i : P * (i + 1), :], windows[i % WINDOWS][:])
 
-        y_scales = keep.tile([P, TILES, T // QUADS], U8, name="y_scales", align_bytes=64)
+        turned, backs, grouped = {}, {}, {}
+        y_scales = held.tile([P, TILES, SPAN], U8, name="y_scales", align_bytes=64)
 
-        grouped, backs = {}, {}
-
-        turned = {}
-
-        def bank_tile(shape, tag):
-            return psum.tile(shape, F32, name=tag, tag=tag, bufs=(2 if tag in ("turned", "back") else 1))
-
-        def turn(i, grp, tag="turned"):
-            window = windows[i % WINDOWS]
+        def turn(i, grp, tag):
             turned[i, grp] = bank_tile([P, QUADS, P], tag)
             for q in range(QUADS):
-                t0 = (T // QUADS) * q + P * grp
-                nc.tensor.transpose(turned[i, grp][:, q, :], window[:, t0 : t0 + P], ident[:])
+                t0 = SPAN * q + P * grp
+                nc.tensor.transpose(turned[i, grp][:, q, :], windows[i % WINDOWS][:, t0 : t0 + P], ident[:])
 
-        def pack(i, grp, copy, tag="back"):
-            half, k = divmod(grp, 2)
+        def pack(i, grp, copy, pairs):
+            pair_of_groups, k = divmod(grp, 2)
             if k == 0:
-                backs[i, half] = bank_tile([P, 2, 2, P], tag)
-            pairs = ring.tile([P, 2 * P], F32, name="pairs", tag="pairs", bufs=4)
+                backs[i, pair_of_groups] = bank_tile([P, 2, 2, P], "back")
             copy(
-                pairs[:].bitcast(BF16).rearrange("p (u m e) -> p u m e", u=2, e=2),
+                pairs.bitcast(BF16).rearrange("p (u m e) -> p u m e", u=2, e=2),
                 turned[i, grp][:].rearrange("p q (m u e) -> p u (q m) e", u=2, e=2),
             )
             for u in range(2):
-                nc.tensor.transpose(backs[i, half][:, k, u, :], pairs[:, P * u : P * (u + 1)], ident[:])
+                nc.tensor.transpose(backs[i, pair_of_groups][:, k, u, :], pairs[:, P * u : P * (u + 1)], ident[:])
 
-        def group(i, half, copy):
-            if half == 0:
-                grouped[i] = ring.tile([P, 2 * HALF], F32, name="grouped", tag="grouped", bufs=2, align_bytes=64)
-            dst = grouped[i][:, HALF * half : HALF * (half + 1)].rearrange("p (k t u) -> p k t u", k=2, u=2)
-            copy(dst, backs[i, half][:].rearrange("p k u t -> p k t u"))
+        def fresh_pairs():
+            pairs = ring.tile([P, 2 * P], F32, name="pairs", tag="pairs", bufs=GROUPS)
+            return pairs[:]
+
+        def group(i, pair_of_groups):
+            if i == LAST:
+                grouped[i] = reset
+            elif pair_of_groups == 0:
+                grouped[i] = ring.tile([P, 2 * SPAN], F32, name="grouped", tag="grouped", bufs=2, align_bytes=64)
+            dst = grouped[i][:, SPAN * pair_of_groups : SPAN * (pair_of_groups + 1)]
+            nc.scalar.copy(
+                dst.rearrange("p (k t u) -> p k t u", k=2, u=2),
+                backs[i, pair_of_groups][:].rearrange("p k u t -> p k t u"),
+            )
 
         words_dram = out_1.rearrange("a p t b -> (a p) (t b)").bitcast(I32)
 
-        def planes(i):
-            y_codes = ring.tile([P, T // QUADS], U32, name="y_codes", tag="y_codes", bufs=3, align_bytes=64)
-            nc.vector.quantize_mx(
-                out=y_codes[:].bitcast(FP8X4), scales=y_scales[:, i, :],
-                in_=grouped[i][:].bitcast(BF16),
-            )
+        def planes(i, y_codes, parts):
+            width = SPAN // parts
+            for c0 in range(0, SPAN, width):
+                nc.vector.quantize_mx(
+                    out=y_codes[:, c0 : c0 + width].bitcast(FP8X4), scales=y_scales[:, i, c0 : c0 + width],
+                    in_=grouped[i][:, 2 * c0 : 2 * (c0 + width)].bitcast(BF16),
+                )
             for q in range(QUADS):
                 nc.sync.dma_start(
-                    words_dram[32 * i : 32 * (i + 1), (T // QUADS) * q : (T // QUADS) * (q + 1)],
-                    y_codes[32 * q : 32 * (q + 1), :].bitcast(I32),
+                    words_dram[QUAD_ROWS * i : QUAD_ROWS * (i + 1), SPAN * q : SPAN * (q + 1)],
+                    y_codes[QUAD_ROWS * q : QUAD_ROWS * (q + 1), :].bitcast(I32),
                 )
 
-        on_scalar, on_vector = nc.scalar.copy, nc.vector.tensor_copy
+        def fresh_codes():
+            y_codes = ring.tile([P, SPAN], U32, name="y_codes", tag="y_codes", bufs=3, align_bytes=64)
+            return y_codes[:]
+
         gather_table(0)
         quantize_x(0)
         turn_biases()
-        for piece in range(4):
+        for piece in range(PASSES * Z):
             round_u(0, piece)
         gate(R, 0, 0)
-        reset(0, 0)
+        apply_reset(0, 0)
         add_message(0, 0)
         candidate(0, 0)
-        round_u(0, 4)
-        round_u(0, 5)
+        for piece in range(PASSES * Z, PIECES):
+            round_u(0, piece)
         gate(Z, 0, 0)
         gather_table(1)
-        second_window = keep.tile([P, T], F32, name="window1", tag="second_window")
-        windows.append(second_window)
-        nc.vector.memset(second_window[:], 0.0)
+        nc.vector.memset(open_window("second_window")[:], 0.0)
         quantize_x(1)
         difference(0, 0)
         damp(0, 0)
-        blend(0, 0)
-        scatter(0, 0)
+        blend(0, 0, mix[:, events(0)])
+        scatter(0, 0, mix[:, events(0)])
         gate(R, 0, 1)
-        reset(0, 1)
+        apply_reset(0, 1)
         add_message(0, 1)
         candidate(0, 1)
         gate(Z, 0, 1)
-        for piece in range(6):
+        for piece in range(PIECES):
             round_u(1, piece)
         difference(0, 1)
         damp(0, 1)
-        blend(0, 1)
+        blend(0, 1, mix[:, events(1)])
         for h in range(HALVES):
             gate(R, 1, h)
-            reset(1, h)
+            apply_reset(1, h)
             add_message(1, h)
             gate(Z, 1, h)
-        for piece in range(6):
+        for piece in range(PIECES):
             round_u(2, piece)
-        load_state(3)
+        load_state(STATES)
+        nc.vector.memset(open_window("third_window")[:], 0.0)
 
-        for i in range(TILES):
-            ahead, nxt, done, coming = i + 2, i + 1, i - 1, i + 3
-            scatter(i, 1 if i == 0 else None)
+        late = held.tile([P, HALF], F32, name="late", tag="late", align_bytes=64)
+
+        def regroup_front(i):
+            turn(i, 0, "turned")
+            turn(i, 1, "turned")
+            pack(i, 0, on_scalar, fresh_pairs())
+            turn(i, 2, "turned")
+            pack(i, 1, on_scalar, fresh_pairs())
+            turn(i, 3, "turned")
+
+        def regroup_back(i):
+            pack(i, 2, on_scalar, fresh_pairs())
+            pack(i, 3, on_scalar, late[:, 0 : 2 * P] if i == LAST - 1 else fresh_pairs())
+            group(i, 0)
+            group(i, 1)
+
+        for i in range(LAST):
+            done, updated, summed, rounded = i - 1, i + 1, i + 2, i + 3
+            left = 1 if i == 0 else None
+            scatter(i, left, mix[:, events(left)])
             store(i)
-            if nxt < TILES:
-                candidate(nxt, 0)
-                candidate(nxt, 1)
-                difference(nxt)
-                if nxt + 3 < TILES:
-                    load_state(nxt + 3)
-            if ahead < TILES:
-                gate(R, ahead, 0)
-                reset(ahead, 0)
-            if nxt < TILES:
-                damp(nxt)
-            if ahead < TILES:
-                gate(Z, ahead, 0)
-                add_message(ahead, 0)
-                gate(R, ahead, 1)
-                reset(ahead, 1)
-            if nxt < TILES:
-                blend(nxt)
-            if ahead < TILES:
-                add_message(ahead, 1)
-            if coming < TILES:
-                round_u(coming, 0)
-            if ahead < TILES:
-                gate(Z, ahead, 1)
-            if coming < TILES:
-                for piece in range(1, 5):
-                    round_u(coming, piece)
+            candidate(updated, 0)
+            candidate(updated, 1)
+            difference(updated, None)
+            if updated + STATES < TILES:
+                load_state(updated + STATES)
+            if summed < TILES:
+                gate(R, summed, 0)
+                apply_reset(summed, 0)
+            damp(updated, None)
+            if summed < TILES:
+                gate(Z, summed, 0)
+                add_message(summed, 0)
+                gate(R, summed, 1)
+                apply_reset(summed, 1)
+            blended = 0 if updated == LAST else None
+            blend(updated, blended, mix[:, events(blended)])
+            if summed < TILES:
+                add_message(summed, 1)
+            if rounded < TILES:
+                round_u(rounded, 0)
+            if summed < TILES:
+                gate(Z, summed, 1)
+            if rounded < TILES:
+                for piece in range(1, PIECES - 1):
+                    round_u(rounded, piece)
             if done >= 0:
-                turn(done, 0)
-                turn(done, 1)
-                pack(done, 0, on_scalar)
-                turn(done, 2)
-                pack(done, 1, on_scalar)
-                turn(done, 3)
-            if coming < TILES:
-                round_u(coming, 5)
+                regroup_front(done)
+            if rounded < TILES:
+                round_u(rounded, PIECES - 1)
             if done >= 0:
-                pack(done, 2, on_scalar)
-                pack(done, 3, on_scalar)
-                group(done, 0, on_scalar)
-                group(done, 1, on_scalar)
-                planes(done)
-        last = TILES - 1
-        turn(last, 0)
-        turn(last, 1)
-        turn(last, 2, "back")
-        turn(last, 3, "back")
-        pack(last, 0, on_scalar, "hn")
-        pack(last, 1, on_vector)
-        pack(last, 2, on_scalar, "xn")
-        pack(last, 3, on_vector)
-        group(last, 0, on_scalar)
-        group(last, 1, on_vector)
-        planes(last)
+                regroup_back(done)
+                if done < LAST - 2:
+                    planes(done, fresh_codes(), 1)
+
+        scatter(LAST, 0, mix[:, events(0)])
+        regroup_front(LAST - 1)
+        regroup_back(LAST - 1)
+        blend(LAST, 1, late[:])
+        scatter(LAST, 1, late[:])
+        store(LAST)
+        late_codes = held.tile([P, 2 * SPAN], U32, name="late_codes", tag="late", align_bytes=64)
+        planes(LAST - 2, late_codes[:, 0:SPAN], 1)
+        planes(LAST - 1, late_codes[:, SPAN:], 1)
+
+        for grp, tag in enumerate(("turned", "turned", "hn", "xn")):
+            turn(LAST, grp, tag)
+        for grp in range(GROUPS):
+            pack(LAST, grp, (on_scalar, on_vector)[grp % 2], fresh_pairs())
+        group(LAST, 0)
+        group(LAST, 1)
+        planes(LAST, fresh_codes(), 2)
+
         scales_dram = out_2.rearrange("a (i r) t -> r (a i) t", r=4)
         for q in range(QUADS):
             nc.scalar.dma_start(
-                scales_dram[:, :, (T // QUADS) * q : (T // QUADS) * (q + 1)].bitcast(I32),
-                y_scales[32 * q : 32 * q + 4, :, :].bitcast(I32),
+                scales_dram[:, :, SPAN * q : SPAN * (q + 1)].bitcast(I32),
+                y_scales[QUAD_ROWS * q : QUAD_ROWS * q + 4, :, :].bitcast(I32),
             )

@@ -76,6 +76,9 @@ def tile_list_tgn_gruP_kernel(
             nc.vector.memset(w_scales[g][:].bitcast(I32), 0)
         bias_rows = held.tile([P, P], F32, name="bias_rows")
         nc.vector.memset(bias_rows[:], 0.0)
+        warm = held.tile([P, 16], F32, name="warm")
+        nc.vector.memset(warm[:, 0:8], 0.0)
+        nc.scalar.activation(out=warm[:, 8:16], in_=warm[:, 0:8], func=ACT.Sigmoid)
 
         table_words = held.tile([P, T], U32, name="table_words", tag="second_window")
         nc.sync.dma_start(table_words[:].bitcast(I32), tab_words[0].rearrange("p t b -> p (t b)").bitcast(I32))

from contextlib import ExitStack

import concourse.mybir as mybir
from concourse.masks import make_identity

K, M, N, T, J = 512, 1024, 1024, 2048, 1024
FLOPS = 2 * 3 * (K + M) * N * J

F32 = mybir.dt.float32
BF16 = mybir.dt.bfloat16
I32 = mybir.dt.int32
U32 = mybir.dt.uint32
U16 = mybir.dt.uint16
U8 = mybir.dt.uint8
FP8X4 = mybir.dt.float8_e4m3fn_x4
FP4X4 = mybir.dt.float4_e2m1fn_x4
ACT = mybir.ActivationFunctionType
ALU = mybir.AluOpType

P = 128
PACK = 4
K_PASS = P * PACK
PASSES = M // K_PASS
HALF = 512
HALVES = J // HALF
TILES = N // P
LAST = TILES - 1
QUADS = 4
QUAD_ROWS = P // QUADS
SPAN = T // QUADS
GROUPS = SPAN // P

R, C, Z = 0, 1, 2
PIECES = 3 * PASSES
U_COLS = PASSES * P

U_CHUNKS = [(0, 128), (128, 128), (256, 256), (512, 256), (768, 256)]
SLOT = 256
W_PARTS = [(0, 256), (256, 256), (512, 512)]
WINDOWS = 3
STATES = 3


def tile_list_tgn_gruP_kernel(
    tc, x, tab_words, tab_scales, wz_words, wz_scales, uz, wr_words, wr_scales, ur,
    wn_words, wn_scales, un, bz, br, bn, hT, wgo, offs, out_0, out_1, out_2,
):
    nc = tc.nc
    w_words_dram = [wr_words, wn_words, wz_words]
    w_scales_dram = [wr_scales, wn_scales, wz_scales]
    u_dram = [ur, un, uz]
    b_dram = [br, bn, bz]
    on_scalar, on_vector = nc.scalar.copy, nc.vector.tensor_copy

    with ExitStack() as ctx:
        held = ctx.enter_context(tc.tile_pool(name="held", bufs=1))
        ring = ctx.enter_context(tc.tile_pool(name="ring", bufs=2))
        psum = ctx.enter_context(tc.psum_pool(name="psum", bufs=1))

        offsets = held.tile([P, J // 16], U16, name="offsets")
        nc.sync.dma_start(offsets[:], offs)

        def events(h):
            return slice(0, J) if h is None else slice(h * HALF, (h + 1) * HALF)

        def list_of(h):
            return offsets[:] if h is None else offsets[:, h * (HALF // 16) : (h + 1) * (HALF // 16)]

        def bank_tile(shape, tag):
            return psum.tile(shape, F32, name=tag, tag=tag, bufs=(2 if tag in ("turned", "back") else 1))

        table_scales = held.tile([P, PASSES, T], U8, name="table_scales", align_bytes=64)
        nc.vector.memset(table_scales[:].rearrange("p a t -> p (a t)").bitcast(I32), 0)
        w_scales = [held.tile([P, N], U8, name="w_scales%d" % g, align_bytes=64) for g in (R, C, Z)]
        for g in (R, C, Z):
            nc.vector.memset(w_scales[g][:].bitcast(I32), 0)
        bias_rows = held.tile([P, P], F32, name="bias_rows")
        nc.vector.memset(bias_rows[:], 0.0)
        warm = held.tile([P, 16], F32, name="warm")
        nc.vector.memset(warm[:, 0:8], 0.0)
        nc.scalar.activation(out=warm[:, 8:16], in_=warm[:, 0:8], func=ACT.Sigmoid)

        table_words = held.tile([P, T], U32, name="table_words", tag="second_window")
        nc.sync.dma_start(table_words[:].bitcast(I32), tab_words[0].rearrange("p t b -> p (t b)").bitcast(I32))
        for q in range(QUADS):
            nc.gpsimd.dma_start(
                table_scales[QUAD_ROWS * q : QUAD_ROWS * q + 4, :, :].bitcast(I32),
                tab_scales[:, 4 * q : 4 * q + 4, :].rearrange("a r t -> r a t").bitcast(I32),
            )
        ident = held.tile([P, P], F32, name="ident")
        make_identity(nc, ident[:])

        def load_w_scales(queue, g, q):
            queue.dma_start(
                w_scales[g][QUAD_ROWS * q : QUAD_ROWS * q + 4, :].bitcast(I32),
                w_scales_dram[g][0, 4 * q : 4 * q + 4, :].bitcast(I32),
            )

        for g in (R, C, Z):
            nc.gpsimd.dma_start(bias_rows[TILES * g : TILES * (g + 1), :], b_dram[g].rearrange("(i p) -> i p", p=P))
        for q in range(QUADS):
            load_w_scales(nc.gpsimd, Z, q)

        windows = []

        def open_window(tag):
            window = held.tile([P, T], F32, name="window%d" % len(windows), tag=tag)
            windows.append(window)
            return window

        nc.vector.memset(open_window("first_window")[:], 0.0)

        x_raw = {}

        def load_x(h):
            x_raw[h] = held.tile([P, PACK, HALF], F32, name="x_raw%d" % h, tag=("x_raw", "third_window")[h])
            nc.sync.dma_start(x_raw[h][:], x[:, events(h)].rearrange("(p t) j -> p t j", t=PACK))

        u_slots = [
            [held.tile([P, PACK * SLOT], F32, name="u_raw%d_%d" % (k, piece)) for piece in range(PIECES)]
            for k in range(2)
        ]

        def u_raw(c, piece):
            n0, width = U_CHUNKS[c]
            e0 = PACK * (n0 % SLOT)
            return u_slots[(n0 // SLOT) % 2][piece][:, e0 : e0 + PACK * width].rearrange("p (t n) -> p t n", t=PACK)

        def load_u(c, piece):
            n0, width = U_CHUNKS[c]
            g, a = divmod(piece, PASSES)
            nc.sync.dma_start(
                u_raw(c, piece),
                u_dram[g][K_PASS * a : K_PASS * (a + 1), n0 : n0 + width].rearrange("(p t) n -> p t n", t=PACK),
            )

        w_words = {}

        def load_w(g, part):
            c0, width = W_PARTS[part]
            w_words[g, part] = held.tile([P, width], U32, name="w_words%d_%d" % (g, part), align_bytes=64)
            flat = w_words_dram[g][0].rearrange("p n b -> p (n b)")
            nc.sync.dma_start(w_words[g, part][:].bitcast(I32), flat[:, PACK * c0 : PACK * (c0 + width)].bitcast(I32))

        state = [held.tile([P, T], F32, name="state%d" % k) for k in range(STATES)]

        def load_state(i):
            nc.sync.dma_start(state[i % STATES][:], hT[P * i : P * (i + 1), :])

        weight = held.tile([P, J], F32, name="weight")

        def load_weight(h):
            nc.sync.dma_start(weight[:, events(h)], wgo[:, events(h)])

        load_x(0)
        load_u(0, 0)
        load_u(0, 1)
        load_w(R, 0)
        load_u(0, 2)
        load_u(0, 3)
        load_w_scales(nc.sync, R, 0)
        load_w(C, 0)
        load_w_scales(nc.sync, R, 1)
        load_state(0)
        load_w_scales(nc.sync, R, 2)
        load_w_scales(nc.sync, R, 3)
        load_u(0, 4)
        load_u(0, 5)
        load_w_scales(nc.sync, C, 0)
        load_w_scales(nc.sync, C, 1)
        load_w_scales(nc.sync, C, 2)
        load_x(1)
        load_w_scales(nc.sync, C, 3)
        load_w(Z, 0)
        load_weight(0)
        for piece in range(PASSES * Z):
            load_u(1, piece)
        load_state(1)
        load_weight(1)
        for piece in range(PASSES * Z, PIECES):
            load_u(1, piece)
        for g in (R, C, Z):
            for a in range(PASSES):
                load_u(2, PASSES * g + a)
            load_w(g, 1)
            if g == C:
                load_state(2)

        v_codes, v_scales, x_codes, x_scales = {}, {}, {}, {}

        def gather_table(h):
            picked = held.tile([P, HALF], U32, name="picked%d" % h)
            nc.vector.tensor_copy(picked[:], table_words[:].indirect(list_of(h)))
            v_codes[h] = held.tile([P, PASSES, 2 * HALF], U8, name="v_codes%d" % h, align_bytes=64)
            nc.vector.tensor_copy(
                v_codes[h][:].bitcast(U16),
                picked[:].bitcast(U16).rearrange("p (j d) -> p d j", d=PASSES),
            )
            for a in range(PASSES):
                v_scales[h, a] = held.tile([P, HALF], U8, name="v_scales%d_%d" % (h, a), align_bytes=64)
                nc.vector.tensor_copy(v_scales[h, a][:], table_scales[:, a, :].indirect(list_of(h)))

        def interleave(dst, raw):
            nc.scalar.copy(
                dst.rearrange("p (c i) t -> p c t i", i=4),
                raw.rearrange("p t (c i) -> p c t i", i=4),
            )

        def quantize_x(h):
            x_bf = ring.tile([P, HALF, PACK], BF16, name="x_bf", tag="x_bf", bufs=1, align_bytes=64)
            interleave(x_bf[:], x_raw[h][:])
            x_codes[h] = held.tile([P, HALF], U32, name="x_codes%d" % h, align_bytes=64)
            x_scales[h] = held.tile([P, HALF], U8, name="x_scales%d" % h, align_bytes=64)
            nc.vector.quantize_mx(
                out=x_codes[h][:].bitcast(FP8X4), scales=x_scales[h][:],
                in_=x_bf[:].rearrange("p j t -> p (j t)"),
            )

        u_bf = [held.tile([P, 3 * U_COLS * PACK], BF16, name="u_bf%d" % k, align_bytes=64) for k in range(2)]
        u_codes = [held.tile([P, 3 * U_COLS], U32, name="u_codes%d" % k, align_bytes=64) for k in range(2)]
        u_scales = [held.tile([P, 3 * U_COLS], U8, name="u_scales%d" % k, align_bytes=64) for k in range(2)]

        def quantize_u(i, g0, g1):
            nc.vector.quantize_mx(
                out=u_codes[i % 2][:, g0 * U_COLS : g1 * U_COLS].bitcast(FP8X4),
                scales=u_scales[i % 2][:, g0 * U_COLS : g1 * U_COLS],
                in_=u_bf[i % 2][:, g0 * U_COLS * PACK : g1 * U_COLS * PACK],
            )

        def round_u(i, piece):
            g, a = divmod(piece, PASSES)
            c = max(k for k, (n0, width) in enumerate(U_CHUNKS) if n0 <= P * i)
            n_off = P * i - U_CHUNKS[c][0]
            c0 = piece * P * PACK
            dst = u_bf[i % 2][:, c0 : c0 + P * PACK].rearrange("p (n t) -> p n t", t=PACK)
            interleave(dst, u_raw(c, piece)[:, :, n_off : n_off + P])
            slot_is_empty = (P * (i + 1)) % SLOT == 0
            if slot_is_empty and c + 2 < len(U_CHUNKS):
                load_u(c + 2, piece)
                if i == 1 and a == PASSES - 1:
                    load_w(g, 2)
            if a == PASSES - 1:
                if i == 0 or g == Z:
                    quantize_u(i, g, g + 1)
                elif g == C:
                    quantize_u(i, R, Z)

        bias = held.tile([P, 3 * TILES], F32, name="bias")

        def turn_biases():
            bank = bank_tile([P, QUADS, P], "turned")
            nc.tensor.transpose(bank[:, 0, :], bias_rows[:], ident[:])
            nc.scalar.copy(bias[:, 0 : Z * TILES], bank[:, 0, 0 : Z * TILES])
            nc.vector.tensor_scalar_mul(bias[:, Z * TILES :], bank[:, 0, Z * TILES : 3 * TILES], -1.0)

        def bias_of(g, i):
            return bias[:, TILES * g + i : TILES * g + i + 1]

        def x_pass(bank, g, i, h, stop):
            part = max(k for k, (n0, width) in enumerate(W_PARTS) if n0 <= P * i)
            c0 = P * i - W_PARTS[part][0]
            nc.tensor.matmul_mx(
                out=bank[:],
                lhsT=w_words[g, part][:, c0 : c0 + P].bitcast(FP8X4),
                lhsT_scale=w_scales[g][:, P * i : P * (i + 1)],
                rhs=x_codes[h][:].bitcast(FP8X4),
                rhs_scale=x_scales[h][:],
                start=True, stop=stop,
            )

        def table_passes(bank, g, i, h, start):
            for a in range(PASSES):
                cols = slice(g * U_COLS + a * P, g * U_COLS + (a + 1) * P)
                nc.tensor.matmul_mx(
                    out=bank[:],
                    lhsT=u_codes[i % 2][:, cols].bitcast(FP8X4),
                    lhsT_scale=u_scales[i % 2][:, cols],
                    rhs=v_codes[h][:, a, :].bitcast(FP4X4),
                    rhs_scale=v_scales[h, a][:],
                    start=(start and a == 0), stop=(a == PASSES - 1),
                )

        cand = [held.tile([P, J], F32, name="cand%d" % k) for k in range(2)]
        mix = held.tile([P, J], F32, name="mix")
        reset = held.tile([P, J], F32, name="reset", align_bytes=64)
        keep = [held.tile([P, J], F32, name="keep%d" % k) for k in range(2)]

        def gate(g, i, h):
            bank = bank_tile([P, HALF], "gate_sum%d" % g)
            x_pass(bank, g, i, h, False)
            table_passes(bank, g, i, h, False)
            dst = reset if g == R else keep[i % 2]
            nc.scalar.activation(
                out=dst[:, events(h)], in_=bank[:], func=ACT.Sigmoid,
                bias=bias_of(g, i), scale=(1.0 if g == R else -1.0),
            )

        def apply_reset(i, h):
            hn = bank_tile([P, HALF], "hn")
            table_passes(hn, C, i, h, True)
            nc.vector.tensor_tensor(cand[i % 2][:, events(h)], hn[:], reset[:, events(h)], ALU.mult)

        def add_message(i, h):
            xn = bank_tile([P, HALF], "xn")
            x_pass(xn, C, i, h, True)
            total = cand[i % 2][:, events(h)]
            nc.vector.tensor_tensor(total, xn[:], total, ALU.add)

        def candidate(i, h):
            total = cand[i % 2][:, events(h)]
            nc.scalar.activation(out=total, in_=total, func=ACT.Tanh, bias=bias_of(C, i))

        def difference(i, h):
            nc.vector.tensor_tensor(
                mix[:, events(h)], state[i % STATES][:].indirect(list_of(h)), cand[i % 2][:, events(h)], ALU.subtract
            )

        def damp(i, h):
            nc.vector.tensor_tensor(mix[:, events(h)], mix[:, events(h)], keep[i % 2][:, events(h)], ALU.mult)

        def blend(i, h, dst):
            nc.vector.tensor_tensor(dst, mix[:, events(h)], cand[i % 2][:, events(h)], ALU.add)

        def scatter(i, h, src):
            nc.vector.tensor_tensor(windows[i % WINDOWS][:].indirect(list_of(h)), src, weight[:, events(h)], ALU.mult)

        def store(i):
            nc.sync.dma_start(out_0[P * i : P * (i + 1), :], windows[i % WINDOWS][:])

        turned, backs, grouped = {}, {}, {}
        y_scales = held.tile([P, TILES, SPAN], U8, name="y_scales", align_bytes=64)

        def turn(i, grp, tag):
            turned[i, grp] = bank_tile([P, QUADS, P], tag)
            for q in range(QUADS):
                t0 = SPAN * q + P * grp
                nc.tensor.transpose(turned[i, grp][:, q, :], windows[i % WINDOWS][:, t0 : t0 + P], ident[:])

        def pack(i, grp, copy, pairs):
            pair_of_groups, k = divmod(grp, 2)
            if k == 0:
                backs[i, pair_of_groups] = bank_tile([P, 2, 2, P], "back")
            copy(
                pairs.bitcast(BF16).rearrange("p (u m e) -> p u m e", u=2, e=2),
                turned[i, grp][:].rearrange("p q (m u e) -> p u (q m) e", u=2, e=2),
            )
            for u in range(2):
                nc.tensor.transpose(backs[i, pair_of_groups][:, k, u, :], pairs[:, P * u : P * (u + 1)], ident[:])

        def fresh_pairs():
            pairs = ring.tile([P, 2 * P], F32, name="pairs", tag="pairs", bufs=GROUPS)
            return pairs[:]

        def group(i, pair_of_groups):
            if i == LAST:
                grouped[i] = reset
            elif pair_of_groups == 0:
                grouped[i] = ring.tile([P, 2 * SPAN], F32, name="grouped", tag="grouped", bufs=2, align_bytes=64)
            dst = grouped[i][:, SPAN * pair_of_groups : SPAN * (pair_of_groups + 1)]
            nc.scalar.copy(
                dst.rearrange("p (k t u) -> p k t u", k=2, u=2),
                backs[i, pair_of_groups][:].rearrange("p k u t -> p k t u"),
            )

        words_dram = out_1.rearrange("a p t b -> (a p) (t b)").bitcast(I32)

        def planes(i, y_codes, parts):
            width = SPAN // parts
            for c0 in range(0, SPAN, width):
                nc.vector.quantize_mx(
                    out=y_codes[:, c0 : c0 + width].bitcast(FP8X4), scales=y_scales[:, i, c0 : c0 + width],
                    in_=grouped[i][:, 2 * c0 : 2 * (c0 + width)].bitcast(BF16),
                )
            for q in range(QUADS):
                nc.sync.dma_start(
                    words_dram[QUAD_ROWS * i : QUAD_ROWS * (i + 1), SPAN * q : SPAN * (q + 1)],
                    y_codes[QUAD_ROWS * q : QUAD_ROWS * (q + 1), :].bitcast(I32),
                )

        def fresh_codes():
            y_codes = ring.tile([P, SPAN], U32, name="y_codes", tag="y_codes", bufs=3, align_bytes=64)
            return y_codes[:]

        gather_table(0)
        quantize_x(0)
        turn_biases()
        for piece in range(PASSES * Z):
            round_u(0, piece)
        gate(R, 0, 0)
        apply_reset(0, 0)
        add_message(0, 0)
        candidate(0, 0)
        for piece in range(PASSES * Z, PIECES):
            round_u(0, piece)
        gate(Z, 0, 0)
        gather_table(1)
        nc.vector.memset(open_window("second_window")[:], 0.0)
        quantize_x(1)
        difference(0, 0)
        damp(0, 0)
        blend(0, 0, mix[:, events(0)])
        scatter(0, 0, mix[:, events(0)])
        gate(R, 0, 1)
        apply_reset(0, 1)
        add_message(0, 1)
        candidate(0, 1)
        gate(Z, 0, 1)
        for piece in range(PIECES):
            round_u(1, piece)
        difference(0, 1)
        damp(0, 1)
        blend(0, 1, mix[:, events(1)])
        for h in range(HALVES):
            gate(R, 1, h)
            apply_reset(1, h)
            add_message(1, h)
            gate(Z, 1, h)
        for piece in range(PIECES):
            round_u(2, piece)
        load_state(STATES)
        nc.vector.memset(open_window("third_window")[:], 0.0)

        late = held.tile([P, HALF], F32, name="late", tag="late", align_bytes=64)

        def regroup_front(i):
            turn(i, 0, "turned")
            turn(i, 1, "turned")
            pack(i, 0, on_scalar, fresh_pairs())
            turn(i, 2, "turned")
            pack(i, 1, on_scalar, fresh_pairs())
            turn(i, 3, "turned")

        def regroup_back(i):
            pack(i, 2, on_scalar, fresh_pairs())
            pack(i, 3, on_scalar, late[:, 0 : 2 * P] if i == LAST - 1 else fresh_pairs())
            group(i, 0)
            group(i, 1)

        for i in range(LAST):
            done, updated, summed, rounded = i - 1, i + 1, i + 2, i + 3
            left = 1 if i == 0 else None
            scatter(i, left, mix[:, events(left)])
            store(i)
            candidate(updated, 0)
            candidate(updated, 1)
            difference(updated, None)
            if updated + STATES < TILES:
                load_state(updated + STATES)
            if summed < TILES:
                gate(R, summed, 0)
                apply_reset(summed, 0)
            damp(updated, None)
            if summed < TILES:
                gate(Z, summed, 0)
                add_message(summed, 0)
                gate(R, summed, 1)
                apply_reset(summed, 1)
            blended = 0 if updated == LAST else None
            blend(updated, blended, mix[:, events(blended)])
            if summed < TILES:
                add_message(summed, 1)
            if rounded < TILES:
                round_u(rounded, 0)
            if summed < TILES:
                gate(Z, summed, 1)
            if rounded < TILES:
                for piece in range(1, PIECES - 1):
                    round_u(rounded, piece)
            if done >= 0:
                regroup_front(done)
            if rounded < TILES:
                round_u(rounded, PIECES - 1)
            if done >= 0:
                regroup_back(done)
                if done < LAST - 2:
                    planes(done, fresh_codes(), 1)

        scatter(LAST, 0, mix[:, events(0)])
        regroup_front(LAST - 1)
        regroup_back(LAST - 1)
        blend(LAST, 1, late[:])
        scatter(LAST, 1, late[:])
        store(LAST)
        late_codes = held.tile([P, 2 * SPAN], U32, name="late_codes", tag="late", align_bytes=64)
        planes(LAST - 2, late_codes[:, 0:SPAN], 1)
        planes(LAST - 1, late_codes[:, SPAN:], 1)

        for grp, tag in enumerate(("turned", "turned", "hn", "xn")):
            turn(LAST, grp, tag)
        for grp in range(GROUPS):
            pack(LAST, grp, (on_scalar, on_vector)[grp % 2], fresh_pairs())
        group(LAST, 0)
        group(LAST, 1)
        planes(LAST, fresh_codes(), 2)

        scales_dram = out_2.rearrange("a (i r) t -> r (a i) t", r=4)
        for q in range(QUADS):
            nc.scalar.dma_start(
                scales_dram[:, :, SPAN * q : SPAN * (q + 1)].bitcast(I32),
                y_scales[QUAD_ROWS * q : QUAD_ROWS * q + 4, :, :].bitcast(I32),
            )
